import numpy as np
import ml_dtypes


def mxq(x, axis, fmt="e4m3"):
    dtype, down = {"e4m3": (ml_dtypes.float8_e4m3fn, 7), "e5m2": (ml_dtypes.float8_e5m2, 14)}[fmt]
    v = np.moveaxis(np.asarray(x, np.float32).astype(ml_dtypes.bfloat16).astype(np.float64), axis, -1)
    blocks = v.reshape(v.shape[:-1] + (-1, 32))
    amax = np.abs(blocks).max(-1, keepdims=True)
    byte = np.maximum(np.where(amax > 0, np.frexp(amax)[1] - 1 + 127, 0) - down, 1)
    scale = np.exp2(byte - 127.0)
    codes = (blocks / scale).astype(np.float32).astype(dtype).astype(np.float64)
    return np.moveaxis((codes * scale).reshape(v.shape), -1, axis)


WIDE = False


def mx_kscale(k):
    if not WIDE:
        return np.ones(k)
    levels = np.array([10, -10, 5, -5, 0])
    if k % 512:
        return np.exp2(np.random.permutation(np.resize(levels, k // 32))).repeat(32)
    a = np.empty((k // 512, 16))
    for p in range(k // 512):
        a[p, :8] = np.random.permutation(np.resize(levels, 8))
        for g in range(8):
            far = levels[np.abs(levels - a[p, g]) >= 10]
            a[p, g + 8] = far[np.random.randint(len(far))]
    return np.exp2(a.ravel()).repeat(32)


BF16 = ml_dtypes.bfloat16


def bf(x):
    return np.asarray(x, np.float32).astype(BF16)


def f64(x):
    return np.asarray(x).astype(np.float64)


E2M1 = np.array([0.0, 0.5, 1.0, 1.5, 2.0, 3.0, 4.0, 6.0, -0.0, -0.5, -1.0, -1.5, -2.0, -3.0, -4.0, -6.0])


def pack_weight(w, fmt):
    k, n = w.shape
    w = f64(bf(w)).reshape(k // 32, 32, n)
    amax = np.abs(w).max(1)
    if fmt == "e4m3":
        byte = np.frexp(amax)[1] - 1 + 127 - 7
    else:
        mant, ex = np.frexp(amax / 6.0)
        byte = np.where(mant > 0.5, ex, ex - 1) + 127
    byte = np.clip(np.where(amax > 0, byte, 1), 1, 254)
    scaled = (w * np.exp2(127.0 - byte)[:, None, :]).reshape(k, n).astype(np.float32)
    by_word = np.ascontiguousarray(scaled.reshape(k // 512, 128, 4, n).transpose(0, 1, 3, 2))
    if fmt == "e4m3":
        words = by_word.astype(ml_dtypes.float8_e4m3fn).view(np.uint8)
    else:
        c = by_word.astype(ml_dtypes.float4_e2m1fn).view(np.uint8) & 0xF
        words = c[..., 0::2] | (c[..., 1::2] << 4)
    return np.ascontiguousarray(words), np.ascontiguousarray(byte.astype(np.uint8).reshape(k // 512, 16, n))


def unpack_weight(words, scales, fmt):
    g, p, n, _ = words.shape
    if fmt == "e4m3":
        vals = np.ascontiguousarray(words).view(ml_dtypes.float8_e4m3fn).astype(np.float64)
    else:
        nib = np.empty((g, p, n, 4), np.uint8)
        nib[..., 0::2] = words & 0xF
        nib[..., 1::2] = words >> 4
        vals = E2M1[nib]
    vals = vals * np.repeat(np.exp2(scales.astype(np.float64) - 127.0), 8, axis=1)[..., None]
    return vals.transpose(0, 1, 3, 2).reshape(g * 512, n)
def pack4(w):
    words, scales = pack_weight(w, "e2m1")
    return words.reshape(words.shape[0], 128, -1), scales


def unpack4(words, scales):
    return unpack_weight(words.reshape(words.shape[0], 128, -1, 2), scales, "e2m1")


def planes(Y):
    n, m = Y.shape
    b = f64(bf(Y)).reshape(n // 32, 32, m)
    amax = np.abs(b).max(1)
    byte = np.clip(np.where(amax > 0, np.frexp(amax)[1] - 1 + 127 - 7, 1), 1, 254)
    codes = (b * np.exp2(127.0 - byte)[:, None, :]).reshape(n, m).astype(np.float32).astype(ml_dtypes.float8_e4m3fn).view(np.uint8)
    words = codes.reshape(n // 512, 128, 4, m).transpose(0, 1, 3, 2)
    return np.ascontiguousarray(words), np.ascontiguousarray(byte.astype(np.uint8).reshape(n // 512, 16, m))


M, K, N = 1536, 1024, 1024


def setup_inputs():
    s = mx_kscale(K)
    c1 = np.random.randn(K, K) / (3 * np.sqrt(K))
    c2 = np.random.randn(K, K) / (3 * np.sqrt(K))
    white = np.random.randn(M, K) * np.exp(0.5 * np.random.randn(M, 1))
    u = np.linalg.solve((np.eye(K) + c2).T, white.T).T
    x = np.linalg.solve((np.eye(K) + c1).T, u.T).T
    probes = np.random.randn(K, N) / np.sqrt(K)
    rate = 0.7 * np.exp(0.4 * np.random.randn(N))
    vote = np.exp(0.8 * np.random.randn(N))
    c1_words, c1_scales = pack4(c1 / s[:, None] * s[None, :])
    return {"x": bf(x * s[None, :]),
            "c1_words": c1_words, "c1_scales": c1_scales,
            "c2": bf(c2 / s[:, None] * s[None, :]),
            "probes": bf(probes / s[:, None]),
            "rate": bf(rate), "vote": bf(vote)}


def reference(x, c1_words, c1_scales, c2, probes, rate, vote):
    x = f64(x)
    c1 = unpack4(c1_words, c1_scales)
    z1 = x + (mxq(x, 1, "e4m3") @ c1)
    z2 = z1 + (mxq(z1, 1, "e4m3") @ mxq(f64(c2), 0, "e4m3"))
    h = mxq(z2, 1, "e4m3") @ mxq(f64(probes), 0, "e4m3")
    keep = np.minimum(1.0, f64(rate) * np.square(h))
    y = keep * f64(vote)
    Y = y.T
    words, scales = planes(Y)
    return y, words, scales

@@ -1,0 +1,506 @@
+from contextlib import ExitStack
+
+import concourse.mybir as mybir
+from concourse.masks import make_identity
+
+M, K, N = 1536, 1024, 1024
+FLOPS = 3 * 2 * M * K * N
+
+F32 = mybir.dt.float32
+BF16 = mybir.dt.bfloat16
+U32 = mybir.dt.uint32
+I32 = mybir.dt.int32
+U8 = mybir.dt.uint8
+FP8X4 = mybir.dt.float8_e4m3fn_x4
+FP4X4 = mybir.dt.float4_e2m1fn_x4
+ALU = mybir.AluOpType
+ACT = mybir.ActivationFunctionType
+
+P = 128
+PACK = 4
+GROUP = P * PACK
+GROUPS = K // GROUP
+TILES = M // P
+BANKS = 8
+BANK_F32 = 512
+CHUNKS = [(0, 4), (4, 4), (8, 2), (10, 2)]
+X_LOADS = [(0, 2), (2, 2), (4, 4), (8, 4)]
+LAG2 = 5
+A = 12
+B = 4
+C = 12
+D = 30
+E = 1
+F = 2
+G = 2
+H = 2
+GP_EARLY = (0, 512)
+GP_LATE = (0, 512, 1024)
+REST_ON_VECTOR = True
+
+
+def tile_probe_leverage_keep_k1_kernel(
+    tc, x, c1_words, c1_scales, c2, probes, rate, vote, out_0, out_1, out_2
+):
+    nc = tc.nc
+    with ExitStack() as ctx:
+        keep = ctx.enter_context(tc.tile_pool(name="keep", bufs=1))
+        work = ctx.enter_context(tc.tile_pool(name="work", bufs=2))
+        psum = ctx.enter_context(tc.psum_pool(name="psum", bufs=1))
+        ctx.enter_context(tc.manual_schedule())
+
+        handed_out = []
+
+        def next_bank():
+            n = len(handed_out)
+            handed_out.append(n)
+            return psum.tile([P, BANK_F32], F32, name="bank%d" % n, tag="bank%d" % (n % BANKS))
+
+        ident = keep.tile([P, P], F32, name="ident")
+        make_identity(nc, ident[:])
+
+        c1s_raw = keep.tile([P, GROUPS, K], U8, name="c1s_raw", align_bytes=64)
+        nc.vector.memset(c1s_raw[:].bitcast(I32), 0)
+
+        x_rows = {}
+
+        def load_x(first, count):
+            rows = keep.tile([P, count, K], BF16, name="x_rows%d" % first)
+            nc.sync.dma_start(
+                out=rows[:], in_=x[first * P : (first + count) * P, :].rearrange("(n p) k -> p n k", p=P)
+            )
+            for n in range(count):
+                x_rows[first + n] = rows[:, n, :]
+
+        w_raw = {}
+
+        def load_w(name, w, g):
+            raw = keep.tile([P, PACK, K], BF16, name="%s_raw%d" % (name, g))
+            nc.sync.dma_start(out=raw[:], in_=w[g * GROUP : (g + 1) * GROUP, :].rearrange("(p j) n -> p j n", j=PACK))
+            w_raw[name, g] = raw
+
+        c1w_raw = keep.tile([P, GROUPS, 2 * K], U8, name="c1w_raw")
+        rate_sb = keep.tile([P, GROUPS, PACK], BF16, name="rate_sb")
+        vote_sb = keep.tile([P, GROUPS, PACK], BF16, name="vote_sb")
+        nc.sync.dma_start(out=c1w_raw[:].bitcast(I32), in_=c1_words.rearrange("g p b -> p g b").bitcast(I32))
+        load_x(*X_LOADS[0])
+        for q in range(4):
+            nc.scalar.dma_start(
+                out=c1s_raw[32 * q : 32 * q + 4, :, :].bitcast(I32),
+                in_=c1_scales[:, 4 * q : 4 * q + 4, :].rearrange("g r n -> r g n").bitcast(I32),
+            )
+        load_w("c2", c2, 0)
+        load_x(*X_LOADS[1])
+        nc.sync.dma_start(out=rate_sb[:], in_=rate.rearrange("(g p t) -> p g t", g=GROUPS, t=PACK))
+        nc.sync.dma_start(out=vote_sb[:], in_=vote.rearrange("(g p t) -> p g t", g=GROUPS, t=PACK))
+        load_w("c2", c2, 1)
+        load_x(*X_LOADS[2])
+        load_w("probes", probes, 0)
+        load_w("probes", probes, 1)
+        load_x(*X_LOADS[3])
+
+        c1_codes = {}
+        c1_scale = {}
+
+        def order_c1(go):
+            for g in range(GROUPS):
+                codes = keep.tile([P, 2 * GROUP], U8, name="c1_codes%d%d" % (g, go), align_bytes=64)
+                nc.vector.tensor_copy(
+                    out=codes[:].rearrange("p (t a m b) -> p a t m b", t=PACK, m=8, b=2),
+                    in_=c1w_raw[:, g, 2 * GROUP * go : 2 * GROUP * (go + 1)].rearrange(
+                        "p (a m t b) -> p a t m b", t=PACK, m=8, b=2
+                    ),
+                )
+                c1_codes[g, go] = codes
+            scale = keep.tile([P, GROUPS, GROUP], U8, name="c1_scale%d" % go, align_bytes=64)
+            nc.vector.tensor_copy(
+                out=scale[:].rearrange("p g (t a m) -> p g a t m", t=PACK, m=16),
+                in_=c1s_raw[:, :, GROUP * go : GROUP * (go + 1)].rearrange("p g (a m t) -> p g a t m", t=PACK, m=16),
+            )
+            c1_scale[go] = scale
+
+        cols = GROUPS * PACK
+        root = keep.tile([P, cols], F32, name="root")
+        cap = keep.tile([P, cols], F32, name="cap")
+        gain = keep.tile([P, cols], F32, name="gain")
+
+        size = keep.tile([P, cols], F32, name="size")
+        safe = keep.tile([P, cols], F32, name="safe")
+        guess = keep.tile([P, cols], F32, name="guess")
+        sgn = keep.tile([P, cols], F32, name="sgn")
+        inv = keep.tile([P, cols], F32, name="inv")
+        half_quot = keep.tile([P, cols], F32, name="half_quot")
+        rate_v = rate_sb[:].rearrange("p g t -> p (g t)")
+        vote_v = vote_sb[:].rearrange("p g t -> p (g t)")
+
+        def constants_a():
+            nc.vector.scalar_tensor_tensor(out=size[:], in0=rate_v, scalar=-1.0, in1=rate_v, op0=ALU.mult, op1=ALU.max)
+
+        def constants_b():
+            nc.vector.tensor_scalar(out=safe[:], in0=size[:], scalar1=1.0e-30, scalar2=None, op0=ALU.max)
+            nc.scalar.activation(out=guess[:], in_=safe[:], func=ACT.Sqrt)
+            nc.scalar.activation(out=sgn[:], in_=rate_v, func=ACT.Sign)
+
+        def constants_c():
+            nc.vector.reciprocal(out=inv[:], in_=guess[:])
+            nc.vector.tensor_scalar(out=cap[:], in0=sgn[:], scalar1=-3.0e38, scalar2=1.0, op0=ALU.mult, op1=ALU.max)
+            nc.vector.tensor_tensor(out=gain[:], in0=vote_v, in1=sgn[:], op=ALU.mult)
+
+        def constants_d():
+            nc.vector.scalar_tensor_tensor(out=half_quot[:], in0=size[:], scalar=0.5, in1=inv[:], op0=ALU.mult, op1=ALU.mult)
+
+        def constants_e():
+            nc.vector.scalar_tensor_tensor(out=root[:], in0=guess[:], scalar=0.5, in1=half_quot[:], op0=ALU.mult, op1=ALU.add)
+
+        w_sorted = {}
+        w_codes = {}
+        w_scale = {}
+
+        def sort_w(name, g, go, half, on_vector):
+            if half == 0:
+                w_sorted[name, g, go] = work.tile(
+                    [P, GROUP * PACK], BF16, name="w_sorted_%s%d%d" % (name, g, go), tag="w_sorted", bufs=3, align_bytes=64
+                )
+            span = slice(32 * half, 32 * half + 32)
+            dst = w_sorted[name, g, go][:].rearrange("p (t a i j) -> p a t i j", t=PACK, i=2, j=PACK)[:, span]
+            src = w_raw[name, g][:, :, GROUP * go : GROUP * (go + 1)].rearrange("p j (a i t) -> p a t i j", t=PACK, i=2)[:, span]
+            if on_vector:
+                nc.vector.tensor_copy(out=dst, in_=src)
+            else:
+                nc.scalar.copy(out=dst, in_=src)
+
+        def quant_w(name, g, go):
+            codes = keep.tile([P, GROUP], U32, name="%s_codes%d%d" % (name, g, go), align_bytes=64)
+            scale = keep.tile([P, GROUP], U8, name="%s_scale%d%d" % (name, g, go), align_bytes=64)
+            nc.vector.quantize_mx(out=codes[:].bitcast(FP8X4), scales=scale[:], in_=w_sorted[name, g, go][:])
+            w_codes[name, g, go] = codes
+            w_scale[name, g, go] = scale
+
+        x_bank = {}
+        x_t = {}
+        x_q = {}
+
+        def turn_x(i):
+            bank = next_bank()
+            words = x_rows[i].bitcast(F32)
+            for g in range(GROUPS):
+                for u in range(2):
+                    n = 2 * g + u
+                    nc.tensor.transpose(bank[:, n * P : (n + 1) * P], words[:, 256 * g + u : 256 * (g + 1) : 2], ident[:])
+            x_bank[i] = bank
+
+        def copy_x(i):
+            xt = work.tile([P, K], BF16, name="x_t%d" % i, tag="x_t", bufs=4, align_bytes=64)
+            nc.scalar.copy(
+                out=xt[:].bitcast(F32).rearrange("p (g r u) -> p g r u", g=GROUPS, u=2),
+                in_=x_bank[i][:].rearrange("p (g u r) -> p g r u", g=GROUPS, u=2),
+            )
+            x_t[i] = xt
+
+        def quant_tile(src, label, i, depth):
+            codes = work.tile([P, GROUPS * P], U32, name="%s_codes%d" % (label, i), tag=label + "_codes", bufs=depth, align_bytes=64)
+            scale = work.tile([P, GROUPS * P], U8, name="%s_scale%d" % (label, i), tag=label + "_scale", bufs=depth, align_bytes=64)
+            nc.vector.quantize_mx(out=codes[:].bitcast(FP8X4), scales=scale[:], in_=src[:])
+            return codes, scale
+
+        def quant_x(i):
+            x_q[i] = quant_tile(x_t[i], "x", i, 4)
+
+        s1_bank = {}
+        z1 = {}
+        z1_bf = {}
+        z1_q = {}
+
+        def mm1(i, go):
+            bank = next_bank()
+            codes, scale = x_q[i]
+            for t in range(PACK):
+                for g in range(GROUPS):
+                    nc.tensor.matmul_mx(
+                        out=bank[:, t * P : (t + 1) * P],
+                        lhsT=c1_codes[g, go][:, 2 * t * P : 2 * (t + 1) * P].bitcast(FP4X4),
+                        lhsT_scale=c1_scale[go][:, g, t * P : (t + 1) * P],
+                        rhs=codes[:, g * P : (g + 1) * P].bitcast(FP8X4),
+                        rhs_scale=scale[:, g * P : (g + 1) * P],
+                        start=(g == 0),
+                        stop=(g == GROUPS - 1),
+                    )
+            s1_bank[i, go] = bank
+
+        def add1(i, go):
+            if go == 0:
+                z1[i] = work.tile([P, K], F32, name="z1_%d" % i, tag="z1", bufs=LAG2 + 2)
+            span = slice(go * GROUP, (go + 1) * GROUP)
+            nc.vector.tensor_tensor(
+                out=z1[i][:, span].rearrange("p (r t) -> p r t", t=PACK),
+                in0=s1_bank[i, go][:].rearrange("p (t r) -> p r t", t=PACK),
+                in1=x_t[i][:, span].rearrange("p (r t) -> p r t", t=PACK),
+                op=ALU.add,
+            )
+
+        def round1(i, lo, hi, on_gpsimd):
+            if lo == 0:
+                z1_bf[i] = work.tile([P, K], BF16, name="z1_bf%d" % i, tag="z1_bf", bufs=3, align_bytes=64)
+            if on_gpsimd:
+                nc.gpsimd.tensor_scalar(
+                    out=z1_bf[i][:, lo:hi], in0=z1[i][:, lo:hi], scalar1=1.0, scalar2=0.0, op0=ALU.mult, op1=ALU.add
+                )
+            elif REST_ON_VECTOR:
+                nc.vector.tensor_copy(out=z1_bf[i][:, lo:hi], in_=z1[i][:, lo:hi])
+            else:
+                nc.scalar.copy(out=z1_bf[i][:, lo:hi], in_=z1[i][:, lo:hi])
+
+        def quant1(i):
+            z1_q[i] = quant_tile(z1_bf[i], "z1", i, LAG2 + 2)
+
+        s2_bank = {}
+        z2_bf = {}
+        z2_q = {}
+        chunk_of = {}
+        for c, (first, count) in enumerate(CHUNKS):
+            for n in range(count):
+                chunk_of[first + n] = c
+
+        def mm2(i, go):
+            bank = next_bank()
+            codes, scale = z1_q[i]
+            for t in range(PACK):
+                for g in range(GROUPS):
+                    nc.tensor.matmul_mx(
+                        out=bank[:, t * P : (t + 1) * P],
+                        lhsT=w_codes["c2", g, go][:, t * P : (t + 1) * P].bitcast(FP8X4),
+                        lhsT_scale=w_scale["c2", g, go][:, t * P : (t + 1) * P],
+                        rhs=codes[:, g * P : (g + 1) * P].bitcast(FP8X4),
+                        rhs_scale=scale[:, g * P : (g + 1) * P],
+                        start=(g == 0),
+                        stop=(g == GROUPS - 1),
+                    )
+            s2_bank[i, go] = bank
+
+        def add2(i, go):
+            z = work.tile([P, GROUP], BF16, name="z2_bf%d_%d" % (i, go), tag="z2_bf", bufs=4, align_bytes=64)
+            nc.vector.tensor_tensor(
+                out=z[:].rearrange("p (r t) -> p r t", t=PACK),
+                in0=s2_bank[i, go][:].rearrange("p (t r) -> p r t", t=PACK),
+                in1=z1[i][:, go * GROUP : (go + 1) * GROUP].rearrange("p (r t) -> p r t", t=PACK),
+                op=ALU.add,
+            )
+            z2_bf[i, go] = z
+
+        def quant2(i, g):
+            c = chunk_of[i]
+            first, count = CHUNKS[c]
+            if i == first:
+                codes = work.tile([P, count * P], U32, name="z2_codes%d_%d" % (c, g), tag="z2_codes", bufs=6, align_bytes=64)
+                scale = work.tile([P, count * P], U8, name="z2_scale%d_%d" % (c, g), tag="z2_scale", bufs=6, align_bytes=64)
+                z2_q[c, g] = (codes, scale)
+            codes, scale = z2_q[c, g]
+            span = slice((i - first) * P, (i - first + 1) * P)
+            nc.vector.quantize_mx(out=codes[:, span].bitcast(FP8X4), scales=scale[:, span], in_=z2_bf[i, g][:])
+
+        s3_bank = {}
+        energy = {}
+        y_t = {}
+        y_bf = {}
+        y_bank = {}
+        y_rows = {}
+        y_scale = keep.tile([P, GROUPS, M], U8, name="y_scale", align_bytes=64)
+
+        def slots(c, h):
+            per_bank = BANK_F32 // (CHUNKS[c][1] * P)
+            return [divmod(s, PACK) for s in range(h * per_bank, (h + 1) * per_bank)]
+
+        def mm3(c, h):
+            width = CHUNKS[c][1] * P
+            bank = next_bank()
+            for n, (go, t) in enumerate(slots(c, h)):
+                for g in range(GROUPS):
+                    codes, scale = z2_q[c, g]
+                    nc.tensor.matmul_mx(
+                        out=bank[:, n * width : (n + 1) * width],
+                        lhsT=w_codes["probes", g, go][:, t * P : (t + 1) * P].bitcast(FP8X4),
+                        lhsT_scale=w_scale["probes", g, go][:, t * P : (t + 1) * P],
+                        rhs=codes[:].bitcast(FP8X4),
+                        rhs_scale=scale[:],
+                        start=(g == 0),
+                        stop=(g == GROUPS - 1),
+                    )
+            s3_bank[c, h] = bank
+
+        def square(c, h):
+            width = CHUNKS[c][1] * P
+            e = work.tile([P, BANK_F32], F32, name="energy%d_%d" % (c, h), tag="energy", bufs=4)
+            for n, (go, t) in enumerate(slots(c, h)):
+                col = go * PACK + t
+                span = slice(n * width, (n + 1) * width)
+                nc.scalar.activation(out=e[:, span], in_=s3_bank[c, h][:, span], func=ACT.Square, scale=root[:, col : col + 1])
+            energy[c, h] = e
+
+        def weigh(c, h):
+            width = CHUNKS[c][1] * P
+            for n, (go, t) in enumerate(slots(c, h)):
+                if t == 0:
+                    y_t[c, go] = work.tile([P, PACK, width], F32, name="y_t%d_%d" % (c, go), tag="y_t", bufs=3)
+                col = go * PACK + t
+                nc.vector.tensor_scalar(
+                    out=y_t[c, go][:, t, :],
+                    in0=energy[c, h][:, n * width : (n + 1) * width],
+                    scalar1=cap[:, col : col + 1],
+                    scalar2=gain[:, col : col + 1],
+                    op0=ALU.min,
+                    op1=ALU.mult,
+                )
+
+        def round_y(i, go, on_vector):
+            c = chunk_of[i]
+            first, count = CHUNKS[c]
+            if (c, go) not in y_bf:
+                y_bf[c, go] = work.tile([P, count * GROUP], BF16, name="y_bf%d_%d" % (c, go), tag="y_bf", bufs=2, align_bytes=64)
+            n = i - first
+            dst = y_bf[c, go][:, n * GROUP : (n + 1) * GROUP].rearrange("p (a i t) -> p a t i", t=PACK, i=4)
+            src = y_t[c, go][:, :, n * P : (n + 1) * P].rearrange("p t (a i) -> p a t i", i=4)
+            if on_vector:
+                nc.vector.tensor_copy(out=dst, in_=src)
+            else:
+                nc.scalar.copy(out=dst, in_=src)
+
+        def quant_y(c, go):
+            first, count = CHUNKS[c]
+            span = slice(first * P, (first + count) * P)
+            codes = work.tile([P, count * P], U32, name="y_codes%d_%d" % (c, go), tag="y_codes", bufs=3, align_bytes=64)
+            nc.vector.quantize_mx(out=codes[:].bitcast(FP8X4), scales=y_scale[:, go, span], in_=y_bf[c, go][:])
+            nc.sync.dma_start(
+                out=out_1[go, :, span, :].rearrange("p m t -> p (m t)").bitcast(I32), in_=codes[:].bitcast(I32)
+            )
+
+        def turn_y(i, go):
+            c = chunk_of[i]
+            n = i - CHUNKS[c][0]
+            bank = next_bank()
+            for t in range(PACK):
+                nc.tensor.transpose(bank[:, t * P : (t + 1) * P], y_t[c, go][:, t, n * P : (n + 1) * P], ident[:])
+            y_bank[i, go] = bank
+
+        def copy_y(i, go, on_vector):
+            rows = work.tile([P, GROUP], F32, name="y_rows%d_%d" % (i, go), tag="y_rows", bufs=4)
+            dst = rows[:].rearrange("p (m t) -> p m t", t=PACK)
+            src = y_bank[i, go][:].rearrange("p (t m) -> p m t", t=PACK)
+            if on_vector:
+                nc.vector.tensor_copy(out=dst, in_=src)
+            else:
+                nc.scalar.copy(out=dst, in_=src)
+            nc.sync.dma_start(out=out_0[i * P : (i + 1) * P, go * GROUP : (go + 1) * GROUP], in_=rows[:])
+
+        c2_jobs = [("c2", g, go) for g in range(GROUPS) for go in range(GROUPS)]
+        probe_jobs = [("probes", g, go) for go in range(GROUPS) for g in range(GROUPS)]
+        halves = [job + (half,) for job in c2_jobs + probe_jobs for half in range(2)]
+        constants = [constants_a, constants_b, constants_c, constants_d, constants_e]
+        to_multiply = [(c, h) for c in range(len(CHUNKS)) for h in range(2 * CHUNKS[c][1])]
+        to_weigh = []
+        to_turn = []
+        to_round = []
+        sorted_in = {}
+        to_quant_y = []
+        quantised2 = set()
+        rest = []
+
+        order_c1(0)
+        for i in range(2):
+            turn_x(i)
+            copy_x(i)
+        quant_x(0)
+        order_c1(1)
+
+        r = 0
+        while to_multiply or to_weigh or to_turn or to_round or to_quant_y:
+            j = r - LAG2
+            if r + 1 < TILES:
+                quant_x(r + 1)
+            for job in rest:
+                round1(*job)
+            rest = []
+            for c, go in to_quant_y:
+                quant_y(c, go)
+            to_quant_y = []
+            if 0 <= j - 1 < TILES:
+                for g in range(GROUPS):
+                    quant2(j - 1, g)
+            if r < len(constants):
+                constants[r]()
+            turn_now = (B if r > A else 2)
+            turning = to_turn[:turn_now]
+            to_turn = to_turn[turn_now:]
+            round_now = (B if r > A else 2)
+            rounding = to_round[:round_now]
+            to_round = to_round[round_now:]
+            for c, h in to_weigh:
+                weigh(c, h)
+                go, t = slots(c, h)[-1]
+                if t == PACK - 1:
+                    first, count = CHUNKS[c]
+                    to_turn.extend((first + n, go) for n in range(count))
+                    to_round.extend((first + n, go) for n in range(count))
+            to_weigh = []
+            for n, (i, go) in enumerate(rounding):
+                if (r >= C or n >= E):
+                    round_y(i, go, True)
+            for job in sorted_in.get(r - G, []):
+                quant_w(*job)
+            if 0 <= r - 1 < TILES:
+                quant1(r - 1)
+            if r + 2 < TILES:
+                turn_x(r + 2)
+            for i, go in turning:
+                turn_y(i, go)
+            if r + 2 < TILES:
+                copy_x(r + 2)
+            for n, (i, go) in enumerate(turning):
+                copy_y(i, go, (r >= D and n == 0))
+            for n in range((B if r >= A else 2)):
+                if to_multiply:
+                    c, h = to_multiply[0]
+                    if sum(CHUNKS[c]) - 1 in quantised2 and ("probes", 1, slots(c, h)[-1][0]) in w_codes:
+                        to_multiply = to_multiply[1:]
+                        mm3(c, h)
+                        square(c, h)
+                        to_weigh.append((c, h))
+            if r < TILES:
+                for go in range(GROUPS):
+                    mm1(r, go)
+            if 0 <= j < TILES:
+                for go in range(GROUPS):
+                    mm2(j, go)
+            if r < TILES:
+                for go in range(GROUPS):
+                    add1(r, go)
+            if 0 <= j < TILES:
+                for go in range(GROUPS):
+                    add2(j, go)
+            if r < TILES:
+                cuts = GP_LATE if j >= 0 else GP_EARLY
+                for n in range(len(cuts) - 1):
+                    round1(r, cuts[n], cuts[n + 1], True)
+                if cuts[-1] < K:
+                    if REST_ON_VECTOR:
+                        rest.append((r, cuts[-1], K, False))
+                    else:
+                        round1(r, cuts[-1], K, False)
+            for n, (i, go) in enumerate(rounding):
+                if not ((r >= C or n >= E)):
+                    round_y(i, go, False)
+                if i + 1 == sum(CHUNKS[chunk_of[i]]):
+                    to_quant_y.append((chunk_of[i], go))
+            sort_now = (F if len(halves) > 4 else H)
+            for job in halves[:sort_now]:
+                sort_w(*job, False)
+                if job[3] == 1:
+                    sorted_in.setdefault(r, []).append(job[:3])
+            halves = halves[sort_now:]
+            quantised2.add(j - 1)
+            r = r + 1
+
+        for q in range(4):
+            nc.sync.dma_start(
+                out=out_2[:, 4 * q : 4 * q + 4, :].rearrange("g r m -> r g m").bitcast(I32),
+                in_=y_scale[32 * q : 32 * q + 4, :, :].bitcast(I32),
+            )

@@ -23,17 +23,20 @@ GROUPS = K // GROUP
 TILES = M // P
 BANKS = 8
 BANK_F32 = 512
-CHUNKS = [(0, 4), (4, 4), (8, 2), (10, 2)]
-X_LOADS = [(0, 2), (2, 2), (4, 4), (8, 4)]
+CHUNKS = [(0, 2), (2, 2), (4, 2), (6, 2), (8, 2), (10, 2)]
+X_LOADS = [(0, 1), (1, 2), (3, 2), (5, 3), (8, 4)]
 LAG2 = 5
 A = 12
 B = 4
 C = 12
 D = 30
-E = 1
+E = 0
 F = 2
-G = 2
+G = 1
 H = 2
+I = 0
+J = 4
+QA = 0
 GP_EARLY = (0, 512)
 GP_LATE = (0, 512, 1024)
 REST_ON_VECTOR = True
@@ -82,6 +85,7 @@ def tile_probe_leverage_keep_k1_kernel(
         c1w_raw = keep.tile([P, GROUPS, 2 * K], U8, name="c1w_raw")
         rate_sb = keep.tile([P, GROUPS, PACK], BF16, name="rate_sb")
         vote_sb = keep.tile([P, GROUPS, PACK], BF16, name="vote_sb")
+        nc.sync.dma_start(out=rate_sb[:], in_=rate.rearrange("(g p t) -> p g t", g=GROUPS, t=PACK))
         nc.sync.dma_start(out=c1w_raw[:].bitcast(I32), in_=c1_words.rearrange("g p b -> p g b").bitcast(I32))
         load_x(*X_LOADS[0])
         for q in range(4):
@@ -89,29 +93,30 @@ def tile_probe_leverage_keep_k1_kernel(
                 out=c1s_raw[32 * q : 32 * q + 4, :, :].bitcast(I32),
                 in_=c1_scales[:, 4 * q : 4 * q + 4, :].rearrange("g r n -> r g n").bitcast(I32),
             )
-        load_w("c2", c2, 0)
         load_x(*X_LOADS[1])
-        nc.sync.dma_start(out=rate_sb[:], in_=rate.rearrange("(g p t) -> p g t", g=GROUPS, t=PACK))
+        load_w("c2", c2, 0)
         nc.sync.dma_start(out=vote_sb[:], in_=vote.rearrange("(g p t) -> p g t", g=GROUPS, t=PACK))
-        load_w("c2", c2, 1)
         load_x(*X_LOADS[2])
+        load_w("c2", c2, 1)
+        load_x(*X_LOADS[3])
         load_w("probes", probes, 0)
         load_w("probes", probes, 1)
-        load_x(*X_LOADS[3])
+        load_x(*X_LOADS[4])
 
         c1_codes = {}
         c1_scale = {}
 
-        def order_c1(go):
-            for g in range(GROUPS):
-                codes = keep.tile([P, 2 * GROUP], U8, name="c1_codes%d%d" % (g, go), align_bytes=64)
-                nc.vector.tensor_copy(
-                    out=codes[:].rearrange("p (t a m b) -> p a t m b", t=PACK, m=8, b=2),
-                    in_=c1w_raw[:, g, 2 * GROUP * go : 2 * GROUP * (go + 1)].rearrange(
-                        "p (a m t b) -> p a t m b", t=PACK, m=8, b=2
-                    ),
-                )
-                c1_codes[g, go] = codes
+        def order_c1_codes(g, go):
+            codes = keep.tile([P, 2 * GROUP], U8, name="c1_codes%d%d" % (g, go), align_bytes=64)
+            nc.vector.tensor_copy(
+                out=codes[:].rearrange("p (t a m b) -> p a t m b", t=PACK, m=8, b=2),
+                in_=c1w_raw[:, g, 2 * GROUP * go : 2 * GROUP * (go + 1)].rearrange(
+                    "p (a m t b) -> p a t m b", t=PACK, m=8, b=2
+                ),
+            )
+            c1_codes[g, go] = codes
+
+        def order_c1_scale(go):
             scale = keep.tile([P, GROUPS, GROUP], U8, name="c1_scale%d" % go, align_bytes=64)
             nc.vector.tensor_copy(
                 out=scale[:].rearrange("p g (t a m) -> p g a t m", t=PACK, m=16),
@@ -359,7 +364,9 @@ def tile_probe_leverage_keep_k1_kernel(
             n = i - first
             dst = y_bf[c, go][:, n * GROUP : (n + 1) * GROUP].rearrange("p (a i t) -> p a t i", t=PACK, i=4)
             src = y_t[c, go][:, :, n * P : (n + 1) * P].rearrange("p t (a i) -> p a t i", i=4)
-            if on_vector:
+            if on_vector == 2:
+                nc.gpsimd.tensor_scalar(out=dst, in0=src, scalar1=1.0, scalar2=1.0, op0=ALU.mult, op1=ALU.mult)
+            elif on_vector:
                 nc.vector.tensor_copy(out=dst, in_=src)
             else:
                 nc.scalar.copy(out=dst, in_=src)
@@ -382,7 +389,7 @@ def tile_probe_leverage_keep_k1_kernel(
             y_bank[i, go] = bank
 
         def copy_y(i, go, on_vector):
-            rows = work.tile([P, GROUP], F32, name="y_rows%d_%d" % (i, go), tag="y_rows", bufs=4)
+            rows = work.tile([P, GROUP], F32, name="y_rows%d_%d" % (i, go), tag="y_rows", bufs=7)
             dst = rows[:].rearrange("p (m t) -> p m t", t=PACK)
             src = y_bank[i, go][:].rearrange("p (t m) -> p m t", t=PACK)
             if on_vector:
@@ -394,60 +401,80 @@ def tile_probe_leverage_keep_k1_kernel(
         c2_jobs = [("c2", g, go) for g in range(GROUPS) for go in range(GROUPS)]
         probe_jobs = [("probes", g, go) for go in range(GROUPS) for g in range(GROUPS)]
         halves = [job + (half,) for job in c2_jobs + probe_jobs for half in range(2)]
-        constants = [constants_a, constants_b, constants_c, constants_d, constants_e]
+        constants = [constants_c, constants_d, constants_e]
         to_multiply = [(c, h) for c in range(len(CHUNKS)) for h in range(2 * CHUNKS[c][1])]
         to_weigh = []
         to_turn = []
         to_round = []
         sorted_in = {}
+        rounded = {}
         to_quant_y = []
-        quantised2 = set()
         rest = []
 
-        order_c1(0)
+        def rounded_y(i, go, where):
+            round_y(i, go, where)
+            c = chunk_of[i]
+            rounded[c, go] = rounded.get((c, go), 0) + 1
+            if rounded[c, go] == CHUNKS[c][1]:
+                to_quant_y.append((c, go))
+
+        constants_a()
+        order_c1_codes(0, 0)
+        constants_b()
+        order_c1_codes(1, 0)
+        order_c1_scale(0)
         for i in range(2):
             turn_x(i)
             copy_x(i)
+        order_c1_codes(0, 1)
         quant_x(0)
-        order_c1(1)
+        order_c1_codes(1, 1)
+        order_c1_scale(1)
 
         r = 0
         while to_multiply or to_weigh or to_turn or to_round or to_quant_y:
             j = r - LAG2
             if r + 1 < TILES:
                 quant_x(r + 1)
+            if 0 <= j - 1 < TILES:
+                quant2(j - 1, 0)
             for job in rest:
                 round1(*job)
             rest = []
             for c, go in to_quant_y:
                 quant_y(c, go)
-            to_quant_y = []
-            if 0 <= j - 1 < TILES:
-                for g in range(GROUPS):
-                    quant2(j - 1, g)
+            to_quant_y.clear()
             if r < len(constants):
                 constants[r]()
+            if 0 <= j - 1 < TILES and QA == 0:
+                quant2(j - 1, 1)
             turn_now = (B if r > A else 2)
             turning = to_turn[:turn_now]
             to_turn = to_turn[turn_now:]
-            round_now = (B if r > A else 2)
-            rounding = to_round[:round_now]
-            to_round = to_round[round_now:]
+            on_v = (J if r >= C else E)
+            on_s = (0 if r >= C else 2 - E)
+            for i, go in to_round[:on_v]:
+                rounded_y(i, go, True)
+            to_round = to_round[on_v:]
+            if 0 <= j - 1 < TILES and QA == 1:
+                quant2(j - 1, 1)
+            s_round = to_round[:on_s]
+            to_round = to_round[on_s:]
+            for job in sorted_in.get(r - G, []):
+                quant_w(*job)
+            if 0 <= r - 1 < TILES:
+                quant1(r - 1)
             for c, h in to_weigh:
                 weigh(c, h)
                 go, t = slots(c, h)[-1]
                 if t == PACK - 1:
                     first, count = CHUNKS[c]
                     to_turn.extend((first + n, go) for n in range(count))
-                    to_round.extend((first + n, go) for n in range(count))
+                    on_g = I if j < TILES else 0
+                    for n in range(on_g):
+                        rounded_y(first + n, go, 2)
+                    to_round.extend((first + n, go) for n in range(on_g, count))
             to_weigh = []
-            for n, (i, go) in enumerate(rounding):
-                if (r >= C or n >= E):
-                    round_y(i, go, True)
-            for job in sorted_in.get(r - G, []):
-                quant_w(*job)
-            if 0 <= r - 1 < TILES:
-                quant1(r - 1)
             if r + 2 < TILES:
                 turn_x(r + 2)
             for i, go in turning:
@@ -456,20 +483,19 @@ def tile_probe_leverage_keep_k1_kernel(
                 copy_x(r + 2)
             for n, (i, go) in enumerate(turning):
                 copy_y(i, go, (r >= D and n == 0))
-            for n in range((B if r >= A else 2)):
-                if to_multiply:
-                    c, h = to_multiply[0]
-                    if sum(CHUNKS[c]) - 1 in quantised2 and ("probes", 1, slots(c, h)[-1][0]) in w_codes:
-                        to_multiply = to_multiply[1:]
-                        mm3(c, h)
-                        square(c, h)
-                        to_weigh.append((c, h))
             if r < TILES:
                 for go in range(GROUPS):
                     mm1(r, go)
             if 0 <= j < TILES:
                 for go in range(GROUPS):
                     mm2(j, go)
+            for n in range((B if r >= A else 2)):
+                if to_multiply:
+                    c, h = to_multiply[0]
+                    if sum(CHUNKS[c]) <= j and ("probes", 1, slots(c, h)[-1][0]) in w_codes:
+                        to_multiply = to_multiply[1:]
+                        mm3(c, h)
+                        to_weigh.append((c, h))
             if r < TILES:
                 for go in range(GROUPS):
                     add1(r, go)
@@ -485,18 +511,16 @@ def tile_probe_leverage_keep_k1_kernel(
                         rest.append((r, cuts[-1], K, False))
                     else:
                         round1(r, cuts[-1], K, False)
-            for n, (i, go) in enumerate(rounding):
-                if not ((r >= C or n >= E)):
-                    round_y(i, go, False)
-                if i + 1 == sum(CHUNKS[chunk_of[i]]):
-                    to_quant_y.append((chunk_of[i], go))
+            for i, go in s_round:
+                rounded_y(i, go, False)
             sort_now = (F if len(halves) > 4 else H)
             for job in halves[:sort_now]:
                 sort_w(*job, False)
                 if job[3] == 1:
                     sorted_in.setdefault(r, []).append(job[:3])
             halves = halves[sort_now:]
-            quantised2.add(j - 1)
+            for c, h in to_weigh:
+                square(c, h)
             r = r + 1
 
         for q in range(4):

@@ -4,7 +4,7 @@ import concourse.mybir as mybir
 from concourse.masks import make_identity
 
 M, K, N = 1536, 1024, 1024
-FLOPS = 3 * 2 * M * K * N
+FLOPS = 2 * M * K * (K + K + N)
 
 F32 = mybir.dt.float32
 BF16 = mybir.dt.bfloat16
@@ -17,29 +17,25 @@ ALU = mybir.AluOpType
 ACT = mybir.ActivationFunctionType
 
 P = 128
-PACK = 4
-GROUP = P * PACK
+SLOTS = 4
+GROUP = P * SLOTS
 GROUPS = K // GROUP
 TILES = M // P
 BANKS = 8
 BANK_F32 = 512
-CHUNKS = [(0, 2), (2, 2), (4, 2), (6, 2), (8, 2), (10, 2)]
+QUADRANTS = 4
+PAIR = 2
+PAIR_TOKENS = PAIR * P
+PAIRS = TILES // PAIR
 X_LOADS = [(0, 1), (1, 2), (3, 2), (5, 3), (8, 4)]
 LAG2 = 5
-A = 12
-B = 4
-C = 12
-D = 30
-E = 0
-F = 2
-G = 1
-H = 2
-I = 0
-J = 4
-QA = 0
-GP_EARLY = (0, 512)
-GP_LATE = (0, 512, 1024)
-REST_ON_VECTOR = True
+TINY = 1.0e-30
+HUGE = 3.0e38
+
+
+def third_round(pair, go):
+    ready = LAG2 + PAIR * pair + PAIR
+    return ready + go if ready < TILES else ready
 
 
 def tile_probe_leverage_keep_k1_kernel(
@@ -52,20 +48,21 @@ def tile_probe_leverage_keep_k1_kernel(
         psum = ctx.enter_context(tc.psum_pool(name="psum", bufs=1))
         ctx.enter_context(tc.manual_schedule())
 
-        handed_out = []
+        banks_taken = []
 
         def next_bank():
-            n = len(handed_out)
-            handed_out.append(n)
+            n = len(banks_taken)
+            banks_taken.append(n)
             return psum.tile([P, BANK_F32], F32, name="bank%d" % n, tag="bank%d" % (n % BANKS))
 
         ident = keep.tile([P, P], F32, name="ident")
         make_identity(nc, ident[:])
 
-        c1s_raw = keep.tile([P, GROUPS, K], U8, name="c1s_raw", align_bytes=64)
-        nc.vector.memset(c1s_raw[:].bitcast(I32), 0)
+        c1_scale_raw = keep.tile([P, GROUPS, K], U8, name="c1_scale_raw", align_bytes=64)
+        nc.vector.memset(c1_scale_raw[:].bitcast(I32), 0)
 
         x_rows = {}
+        w_raw = {}
 
         def load_x(first, count):
             rows = keep.tile([P, count, K], BF16, name="x_rows%d" % first)
@@ -75,27 +72,25 @@ def tile_probe_leverage_keep_k1_kernel(
             for n in range(count):
                 x_rows[first + n] = rows[:, n, :]
 
-        w_raw = {}
-
         def load_w(name, w, g):
-            raw = keep.tile([P, PACK, K], BF16, name="%s_raw%d" % (name, g))
-            nc.sync.dma_start(out=raw[:], in_=w[g * GROUP : (g + 1) * GROUP, :].rearrange("(p j) n -> p j n", j=PACK))
+            raw = keep.tile([P, SLOTS, K], BF16, name="%s_raw%d" % (name, g))
+            nc.sync.dma_start(out=raw[:], in_=w[g * GROUP : (g + 1) * GROUP, :].rearrange("(p j) n -> p j n", j=SLOTS))
             w_raw[name, g] = raw
 
-        c1w_raw = keep.tile([P, GROUPS, 2 * K], U8, name="c1w_raw")
-        rate_sb = keep.tile([P, GROUPS, PACK], BF16, name="rate_sb")
-        vote_sb = keep.tile([P, GROUPS, PACK], BF16, name="vote_sb")
-        nc.sync.dma_start(out=rate_sb[:], in_=rate.rearrange("(g p t) -> p g t", g=GROUPS, t=PACK))
-        nc.sync.dma_start(out=c1w_raw[:].bitcast(I32), in_=c1_words.rearrange("g p b -> p g b").bitcast(I32))
+        c1_word_raw = keep.tile([P, GROUPS, 2 * K], U8, name="c1_word_raw")
+        rate_sb = keep.tile([P, GROUPS, SLOTS], BF16, name="rate_sb")
+        vote_sb = keep.tile([P, GROUPS, SLOTS], BF16, name="vote_sb")
+        nc.sync.dma_start(out=rate_sb[:], in_=rate.rearrange("(g p t) -> p g t", g=GROUPS, t=SLOTS))
+        nc.sync.dma_start(out=c1_word_raw[:].bitcast(I32), in_=c1_words.rearrange("g p b -> p g b").bitcast(I32))
         load_x(*X_LOADS[0])
-        for q in range(4):
+        for q in range(QUADRANTS):
             nc.scalar.dma_start(
-                out=c1s_raw[32 * q : 32 * q + 4, :, :].bitcast(I32),
+                out=c1_scale_raw[32 * q : 32 * q + 4, :, :].bitcast(I32),
                 in_=c1_scales[:, 4 * q : 4 * q + 4, :].rearrange("g r n -> r g n").bitcast(I32),
             )
         load_x(*X_LOADS[1])
         load_w("c2", c2, 0)
-        nc.sync.dma_start(out=vote_sb[:], in_=vote.rearrange("(g p t) -> p g t", g=GROUPS, t=PACK))
+        nc.sync.dma_start(out=vote_sb[:], in_=vote.rearrange("(g p t) -> p g t", g=GROUPS, t=SLOTS))
         load_x(*X_LOADS[2])
         load_w("c2", c2, 1)
         load_x(*X_LOADS[3])
@@ -106,73 +101,75 @@ def tile_probe_leverage_keep_k1_kernel(
         c1_codes = {}
         c1_scale = {}
 
-        def order_c1_codes(g, go):
+        def sort_c1_codes(g, go):
             codes = keep.tile([P, 2 * GROUP], U8, name="c1_codes%d%d" % (g, go), align_bytes=64)
             nc.vector.tensor_copy(
-                out=codes[:].rearrange("p (t a m b) -> p a t m b", t=PACK, m=8, b=2),
-                in_=c1w_raw[:, g, 2 * GROUP * go : 2 * GROUP * (go + 1)].rearrange(
-                    "p (a m t b) -> p a t m b", t=PACK, m=8, b=2
+                out=codes[:].rearrange("p (t a m b) -> p a t m b", t=SLOTS, m=8, b=2),
+                in_=c1_word_raw[:, g, 2 * GROUP * go : 2 * GROUP * (go + 1)].rearrange(
+                    "p (a m t b) -> p a t m b", t=SLOTS, m=8, b=2
                 ),
             )
             c1_codes[g, go] = codes
 
-        def order_c1_scale(go):
+        def sort_c1_scale(go):
             scale = keep.tile([P, GROUPS, GROUP], U8, name="c1_scale%d" % go, align_bytes=64)
             nc.vector.tensor_copy(
-                out=scale[:].rearrange("p g (t a m) -> p g a t m", t=PACK, m=16),
-                in_=c1s_raw[:, :, GROUP * go : GROUP * (go + 1)].rearrange("p g (a m t) -> p g a t m", t=PACK, m=16),
+                out=scale[:].rearrange("p g (t a m) -> p g a t m", t=SLOTS, m=16),
+                in_=c1_scale_raw[:, :, GROUP * go : GROUP * (go + 1)].rearrange(
+                    "p g (a m t) -> p g a t m", t=SLOTS, m=16
+                ),
             )
             c1_scale[go] = scale
 
-        cols = GROUPS * PACK
-        root = keep.tile([P, cols], F32, name="root")
-        cap = keep.tile([P, cols], F32, name="cap")
-        gain = keep.tile([P, cols], F32, name="gain")
+        def probe_tile(name):
+            return keep.tile([P, GROUPS * SLOTS], F32, name=name)
 
-        size = keep.tile([P, cols], F32, name="size")
-        safe = keep.tile([P, cols], F32, name="safe")
-        guess = keep.tile([P, cols], F32, name="guess")
-        sgn = keep.tile([P, cols], F32, name="sgn")
-        inv = keep.tile([P, cols], F32, name="inv")
-        half_quot = keep.tile([P, cols], F32, name="half_quot")
-        rate_v = rate_sb[:].rearrange("p g t -> p (g t)")
-        vote_v = vote_sb[:].rearrange("p g t -> p (g t)")
+        root, cap, gain = probe_tile("root"), probe_tile("cap"), probe_tile("gain")
+        rate_abs, rate_safe, rate_sign = probe_tile("rate_abs"), probe_tile("rate_safe"), probe_tile("rate_sign")
+        guess, inverse, half_quotient = probe_tile("guess"), probe_tile("inverse"), probe_tile("half_quotient")
+        rate_cols = rate_sb[:].rearrange("p g t -> p (g t)")
+        vote_cols = vote_sb[:].rearrange("p g t -> p (g t)")
 
-        def constants_a():
-            nc.vector.scalar_tensor_tensor(out=size[:], in0=rate_v, scalar=-1.0, in1=rate_v, op0=ALU.mult, op1=ALU.max)
+        def take_abs():
+            nc.vector.scalar_tensor_tensor(
+                out=rate_abs[:], in0=rate_cols, scalar=-1.0, in1=rate_cols, op0=ALU.mult, op1=ALU.max
+            )
 
-        def constants_b():
-            nc.vector.tensor_scalar(out=safe[:], in0=size[:], scalar1=1.0e-30, scalar2=None, op0=ALU.max)
-            nc.scalar.activation(out=guess[:], in_=safe[:], func=ACT.Sqrt)
-            nc.scalar.activation(out=sgn[:], in_=rate_v, func=ACT.Sign)
+        def guess_root():
+            nc.vector.tensor_scalar(out=rate_safe[:], in0=rate_abs[:], scalar1=TINY, scalar2=None, op0=ALU.max)
+            nc.scalar.activation(out=guess[:], in_=rate_safe[:], func=ACT.Sqrt)
+            nc.scalar.activation(out=rate_sign[:], in_=rate_cols, func=ACT.Sign)
 
-        def constants_c():
-            nc.vector.reciprocal(out=inv[:], in_=guess[:])
-            nc.vector.tensor_scalar(out=cap[:], in0=sgn[:], scalar1=-3.0e38, scalar2=1.0, op0=ALU.mult, op1=ALU.max)
-            nc.vector.tensor_tensor(out=gain[:], in0=vote_v, in1=sgn[:], op=ALU.mult)
+        def invert_guess_and_sign():
+            nc.vector.reciprocal(out=inverse[:], in_=guess[:])
+            nc.vector.tensor_scalar(out=cap[:], in0=rate_sign[:], scalar1=-HUGE, scalar2=1.0, op0=ALU.mult, op1=ALU.max)
+            nc.vector.tensor_tensor(out=gain[:], in0=vote_cols, in1=rate_sign[:], op=ALU.mult)
 
-        def constants_d():
-            nc.vector.scalar_tensor_tensor(out=half_quot[:], in0=size[:], scalar=0.5, in1=inv[:], op0=ALU.mult, op1=ALU.mult)
+        def newton_quotient():
+            nc.vector.scalar_tensor_tensor(
+                out=half_quotient[:], in0=rate_abs[:], scalar=0.5, in1=inverse[:], op0=ALU.mult, op1=ALU.mult
+            )
 
-        def constants_e():
-            nc.vector.scalar_tensor_tensor(out=root[:], in0=guess[:], scalar=0.5, in1=half_quot[:], op0=ALU.mult, op1=ALU.add)
+        def newton_sum():
+            nc.vector.scalar_tensor_tensor(
+                out=root[:], in0=guess[:], scalar=0.5, in1=half_quotient[:], op0=ALU.mult, op1=ALU.add
+            )
 
         w_sorted = {}
         w_codes = {}
         w_scale = {}
 
-        def sort_w(name, g, go, half, on_vector):
-            if half == 0:
-                w_sorted[name, g, go] = work.tile(
-                    [P, GROUP * PACK], BF16, name="w_sorted_%s%d%d" % (name, g, go), tag="w_sorted", bufs=3, align_bytes=64
-                )
-            span = slice(32 * half, 32 * half + 32)
-            dst = w_sorted[name, g, go][:].rearrange("p (t a i j) -> p a t i j", t=PACK, i=2, j=PACK)[:, span]
-            src = w_raw[name, g][:, :, GROUP * go : GROUP * (go + 1)].rearrange("p j (a i t) -> p a t i j", t=PACK, i=2)[:, span]
-            if on_vector:
-                nc.vector.tensor_copy(out=dst, in_=src)
-            else:
-                nc.scalar.copy(out=dst, in_=src)
+        def sort_w(name, g, go):
+            dst = work.tile(
+                [P, GROUP * SLOTS], BF16, name="w_sorted_%s%d%d" % (name, g, go), tag="w_sorted", bufs=3, align_bytes=64
+            )
+            nc.scalar.copy(
+                out=dst[:].rearrange("p (t a i j) -> p a t i j", t=SLOTS, i=2, j=SLOTS),
+                in_=w_raw[name, g][:, :, GROUP * go : GROUP * (go + 1)].rearrange(
+                    "p j (a i t) -> p a t i j", t=SLOTS, i=2
+                ),
+            )
+            w_sorted[name, g, go] = dst
 
         def quant_w(name, g, go):
             codes = keep.tile([P, GROUP], U32, name="%s_codes%d%d" % (name, g, go), align_bytes=64)
@@ -188,141 +185,144 @@ def tile_probe_leverage_keep_k1_kernel(
         def turn_x(i):
             bank = next_bank()
             words = x_rows[i].bitcast(F32)
+            half = GROUP // 2
             for g in range(GROUPS):
                 for u in range(2):
                     n = 2 * g + u
-                    nc.tensor.transpose(bank[:, n * P : (n + 1) * P], words[:, 256 * g + u : 256 * (g + 1) : 2], ident[:])
+                    nc.tensor.transpose(bank[:, n * P : (n + 1) * P], words[:, half * g + u : half * (g + 1) : 2], ident[:])
             x_bank[i] = bank
 
         def copy_x(i):
-            xt = work.tile([P, K], BF16, name="x_t%d" % i, tag="x_t", bufs=4, align_bytes=64)
+            dst = work.tile([P, K], BF16, name="x_t%d" % i, tag="x_t", bufs=4, align_bytes=64)
             nc.scalar.copy(
-                out=xt[:].bitcast(F32).rearrange("p (g r u) -> p g r u", g=GROUPS, u=2),
+                out=dst[:].bitcast(F32).rearrange("p (g r u) -> p g r u", g=GROUPS, u=2),
                 in_=x_bank[i][:].rearrange("p (g u r) -> p g r u", g=GROUPS, u=2),
             )
-            x_t[i] = xt
+            x_t[i] = dst
 
         def quant_tile(src, label, i, depth):
-            codes = work.tile([P, GROUPS * P], U32, name="%s_codes%d" % (label, i), tag=label + "_codes", bufs=depth, align_bytes=64)
-            scale = work.tile([P, GROUPS * P], U8, name="%s_scale%d" % (label, i), tag=label + "_scale", bufs=depth, align_bytes=64)
+            codes = work.tile(
+                [P, GROUPS * P], U32, name="%s_codes%d" % (label, i), tag=label + "_codes", bufs=depth, align_bytes=64
+            )
+            scale = work.tile(
+                [P, GROUPS * P], U8, name="%s_scale%d" % (label, i), tag=label + "_scale", bufs=depth, align_bytes=64
+            )
             nc.vector.quantize_mx(out=codes[:].bitcast(FP8X4), scales=scale[:], in_=src[:])
             return codes, scale
 
         def quant_x(i):
             x_q[i] = quant_tile(x_t[i], "x", i, 4)
 
-        s1_bank = {}
+        bank1 = {}
+        bank2 = {}
         z1 = {}
         z1_bf = {}
         z1_q = {}
+        z2_bf = {}
+        z2_q = {}
 
-        def mm1(i, go):
+        def multiply_tile(operand, weight, weight_scale):
             bank = next_bank()
-            codes, scale = x_q[i]
-            for t in range(PACK):
+            codes, scale = operand
+            for t in range(SLOTS):
                 for g in range(GROUPS):
                     nc.tensor.matmul_mx(
                         out=bank[:, t * P : (t + 1) * P],
-                        lhsT=c1_codes[g, go][:, 2 * t * P : 2 * (t + 1) * P].bitcast(FP4X4),
-                        lhsT_scale=c1_scale[go][:, g, t * P : (t + 1) * P],
+                        lhsT=weight(g, t),
+                        lhsT_scale=weight_scale(g, t),
                         rhs=codes[:, g * P : (g + 1) * P].bitcast(FP8X4),
                         rhs_scale=scale[:, g * P : (g + 1) * P],
                         start=(g == 0),
                         stop=(g == GROUPS - 1),
                     )
-            s1_bank[i, go] = bank
+            return bank
+
+        def add_residual(dst, bank, residual):
+            nc.vector.tensor_tensor(
+                out=dst.rearrange("p (r t) -> p r t", t=SLOTS),
+                in0=bank[:].rearrange("p (t r) -> p r t", t=SLOTS),
+                in1=residual.rearrange("p (r t) -> p r t", t=SLOTS),
+                op=ALU.add,
+            )
+
+        def multiply1(i, go):
+            bank1[i, go] = multiply_tile(
+                x_q[i],
+                lambda g, t: c1_codes[g, go][:, 2 * t * P : 2 * (t + 1) * P].bitcast(FP4X4),
+                lambda g, t: c1_scale[go][:, g, t * P : (t + 1) * P],
+            )
 
         def add1(i, go):
             if go == 0:
                 z1[i] = work.tile([P, K], F32, name="z1_%d" % i, tag="z1", bufs=LAG2 + 2)
-            span = slice(go * GROUP, (go + 1) * GROUP)
-            nc.vector.tensor_tensor(
-                out=z1[i][:, span].rearrange("p (r t) -> p r t", t=PACK),
-                in0=s1_bank[i, go][:].rearrange("p (t r) -> p r t", t=PACK),
-                in1=x_t[i][:, span].rearrange("p (r t) -> p r t", t=PACK),
-                op=ALU.add,
-            )
-
-        def round1(i, lo, hi, on_gpsimd):
-            if lo == 0:
                 z1_bf[i] = work.tile([P, K], BF16, name="z1_bf%d" % i, tag="z1_bf", bufs=3, align_bytes=64)
-            if on_gpsimd:
+            span = slice(go * GROUP, (go + 1) * GROUP)
+            add_residual(z1[i][:, span], bank1[i, go], x_t[i][:, span])
+
+        def gpsimd_columns(i):
+            return GROUP if i >= LAG2 else 0
+
+        def round1_on_gpsimd(i):
+            for first in range(0, gpsimd_columns(i), GROUP):
+                span = slice(first, first + GROUP)
                 nc.gpsimd.tensor_scalar(
-                    out=z1_bf[i][:, lo:hi], in0=z1[i][:, lo:hi], scalar1=1.0, scalar2=0.0, op0=ALU.mult, op1=ALU.add
+                    out=z1_bf[i][:, span], in0=z1[i][:, span], scalar1=1.0, scalar2=0.0, op0=ALU.mult, op1=ALU.add
                 )
-            elif REST_ON_VECTOR:
-                nc.vector.tensor_copy(out=z1_bf[i][:, lo:hi], in_=z1[i][:, lo:hi])
-            else:
-                nc.scalar.copy(out=z1_bf[i][:, lo:hi], in_=z1[i][:, lo:hi])
+
+        def round1_on_vector(i):
+            nc.vector.tensor_copy(out=z1_bf[i][:, gpsimd_columns(i) :], in_=z1[i][:, gpsimd_columns(i) :])
 
         def quant1(i):
             z1_q[i] = quant_tile(z1_bf[i], "z1", i, LAG2 + 2)
 
-        s2_bank = {}
-        z2_bf = {}
-        z2_q = {}
-        chunk_of = {}
-        for c, (first, count) in enumerate(CHUNKS):
-            for n in range(count):
-                chunk_of[first + n] = c
-
-        def mm2(i, go):
-            bank = next_bank()
-            codes, scale = z1_q[i]
-            for t in range(PACK):
-                for g in range(GROUPS):
-                    nc.tensor.matmul_mx(
-                        out=bank[:, t * P : (t + 1) * P],
-                        lhsT=w_codes["c2", g, go][:, t * P : (t + 1) * P].bitcast(FP8X4),
-                        lhsT_scale=w_scale["c2", g, go][:, t * P : (t + 1) * P],
-                        rhs=codes[:, g * P : (g + 1) * P].bitcast(FP8X4),
-                        rhs_scale=scale[:, g * P : (g + 1) * P],
-                        start=(g == 0),
-                        stop=(g == GROUPS - 1),
-                    )
-            s2_bank[i, go] = bank
+        def multiply2(i, go):
+            bank2[i, go] = multiply_tile(
+                z1_q[i],
+                lambda g, t: w_codes["c2", g, go][:, t * P : (t + 1) * P].bitcast(FP8X4),
+                lambda g, t: w_scale["c2", g, go][:, t * P : (t + 1) * P],
+            )
 
         def add2(i, go):
-            z = work.tile([P, GROUP], BF16, name="z2_bf%d_%d" % (i, go), tag="z2_bf", bufs=4, align_bytes=64)
-            nc.vector.tensor_tensor(
-                out=z[:].rearrange("p (r t) -> p r t", t=PACK),
-                in0=s2_bank[i, go][:].rearrange("p (t r) -> p r t", t=PACK),
-                in1=z1[i][:, go * GROUP : (go + 1) * GROUP].rearrange("p (r t) -> p r t", t=PACK),
-                op=ALU.add,
-            )
-            z2_bf[i, go] = z
+            dst = work.tile([P, GROUP], BF16, name="z2_bf%d_%d" % (i, go), tag="z2_bf", bufs=4, align_bytes=64)
+            add_residual(dst[:], bank2[i, go], z1[i][:, go * GROUP : (go + 1) * GROUP])
+            z2_bf[i, go] = dst
 
         def quant2(i, g):
-            c = chunk_of[i]
-            first, count = CHUNKS[c]
-            if i == first:
-                codes = work.tile([P, count * P], U32, name="z2_codes%d_%d" % (c, g), tag="z2_codes", bufs=6, align_bytes=64)
-                scale = work.tile([P, count * P], U8, name="z2_scale%d_%d" % (c, g), tag="z2_scale", bufs=6, align_bytes=64)
-                z2_q[c, g] = (codes, scale)
-            codes, scale = z2_q[c, g]
-            span = slice((i - first) * P, (i - first + 1) * P)
+            pair, n = divmod(i, PAIR)
+            if n == 0:
+                codes = work.tile(
+                    [P, PAIR_TOKENS], U32, name="z2_codes%d_%d" % (pair, g), tag="z2_codes", bufs=6, align_bytes=64
+                )
+                scale = work.tile(
+                    [P, PAIR_TOKENS], U8, name="z2_scale%d_%d" % (pair, g), tag="z2_scale", bufs=6, align_bytes=64
+                )
+                z2_q[pair, g] = (codes, scale)
+            codes, scale = z2_q[pair, g]
+            span = slice(n * P, (n + 1) * P)
             nc.vector.quantize_mx(out=codes[:, span].bitcast(FP8X4), scales=scale[:, span], in_=z2_bf[i, g][:])
 
-        s3_bank = {}
+        slots_in_bank = BANK_F32 // PAIR_TOKENS
+        bank3 = {}
         energy = {}
         y_t = {}
         y_bf = {}
         y_bank = {}
-        y_rows = {}
-        y_scale = keep.tile([P, GROUPS, M], U8, name="y_scale", align_bytes=64)
+        early = M - PAIR_TOKENS
+        y_scale_early = keep.tile([P, GROUPS, early], U8, name="y_scale_early", align_bytes=64)
+        y_scale_last = keep.tile([P, GROUPS, PAIR_TOKENS], U8, name="y_scale_last", align_bytes=64)
 
-        def slots(c, h):
-            per_bank = BANK_F32 // (CHUNKS[c][1] * P)
-            return [divmod(s, PACK) for s in range(h * per_bank, (h + 1) * per_bank)]
+        def slot_span(t):
+            n = t % slots_in_bank
+            return slice(n * PAIR_TOKENS, (n + 1) * PAIR_TOKENS)
 
-        def mm3(c, h):
-            width = CHUNKS[c][1] * P
-            bank = next_bank()
-            for n, (go, t) in enumerate(slots(c, h)):
+        def multiply3(pair, go):
+            for t in range(SLOTS):
+                if t % slots_in_bank == 0:
+                    bank = next_bank()
                 for g in range(GROUPS):
-                    codes, scale = z2_q[c, g]
+                    codes, scale = z2_q[pair, g]
                     nc.tensor.matmul_mx(
-                        out=bank[:, n * width : (n + 1) * width],
+                        out=bank[:, slot_span(t)],
                         lhsT=w_codes["probes", g, go][:, t * P : (t + 1) * P].bitcast(FP8X4),
                         lhsT_scale=w_scale["probes", g, go][:, t * P : (t + 1) * P],
                         rhs=codes[:].bitcast(FP8X4),
@@ -330,201 +330,163 @@ def tile_probe_leverage_keep_k1_kernel(
                         start=(g == 0),
                         stop=(g == GROUPS - 1),
                     )
-            s3_bank[c, h] = bank
+                bank3[pair, go, t] = bank
 
-        def square(c, h):
-            width = CHUNKS[c][1] * P
-            e = work.tile([P, BANK_F32], F32, name="energy%d_%d" % (c, h), tag="energy", bufs=4)
-            for n, (go, t) in enumerate(slots(c, h)):
-                col = go * PACK + t
-                span = slice(n * width, (n + 1) * width)
-                nc.scalar.activation(out=e[:, span], in_=s3_bank[c, h][:, span], func=ACT.Square, scale=root[:, col : col + 1])
-            energy[c, h] = e
+        def square(pair, go):
+            for t in range(SLOTS):
+                if t % slots_in_bank == 0:
+                    dst = work.tile([P, BANK_F32], F32, name="energy%d_%d_%d" % (pair, go, t), tag="energy", bufs=4)
+                col = go * SLOTS + t
+                nc.scalar.activation(
+                    out=dst[:, slot_span(t)],
+                    in_=bank3[pair, go, t][:, slot_span(t)],
+                    func=ACT.Square,
+                    scale=root[:, col : col + 1],
+                )
+                energy[pair, go, t] = dst
 
-        def weigh(c, h):
-            width = CHUNKS[c][1] * P
-            for n, (go, t) in enumerate(slots(c, h)):
-                if t == 0:
-                    y_t[c, go] = work.tile([P, PACK, width], F32, name="y_t%d_%d" % (c, go), tag="y_t", bufs=3)
-                col = go * PACK + t
+        def weigh(pair, go):
+            dst = work.tile([P, SLOTS, PAIR_TOKENS], F32, name="y_t%d_%d" % (pair, go), tag="y_t", bufs=4)
+            for t in range(SLOTS):
+                col = go * SLOTS + t
                 nc.vector.tensor_scalar(
-                    out=y_t[c, go][:, t, :],
-                    in0=energy[c, h][:, n * width : (n + 1) * width],
+                    out=dst[:, t, :],
+                    in0=energy[pair, go, t][:, slot_span(t)],
                     scalar1=cap[:, col : col + 1],
                     scalar2=gain[:, col : col + 1],
                     op0=ALU.min,
                     op1=ALU.mult,
                 )
+            y_t[pair, go] = dst
 
-        def round_y(i, go, on_vector):
-            c = chunk_of[i]
-            first, count = CHUNKS[c]
-            if (c, go) not in y_bf:
-                y_bf[c, go] = work.tile([P, count * GROUP], BF16, name="y_bf%d_%d" % (c, go), tag="y_bf", bufs=2, align_bytes=64)
-            n = i - first
-            dst = y_bf[c, go][:, n * GROUP : (n + 1) * GROUP].rearrange("p (a i t) -> p a t i", t=PACK, i=4)
-            src = y_t[c, go][:, :, n * P : (n + 1) * P].rearrange("p t (a i) -> p a t i", i=4)
-            if on_vector == 2:
-                nc.gpsimd.tensor_scalar(out=dst, in0=src, scalar1=1.0, scalar2=1.0, op0=ALU.mult, op1=ALU.mult)
-            elif on_vector:
-                nc.vector.tensor_copy(out=dst, in_=src)
-            else:
-                nc.scalar.copy(out=dst, in_=src)
+        def round_y(pair, go, copy):
+            dst = work.tile(
+                [P, PAIR_TOKENS * SLOTS], BF16, name="y_bf%d_%d" % (pair, go), tag="y_bf", bufs=3, align_bytes=64
+            )
+            copy(
+                out=dst[:].rearrange("p (a i t) -> p a t i", t=SLOTS, i=4),
+                in_=y_t[pair, go][:].rearrange("p t (a i) -> p a t i", i=4),
+            )
+            y_bf[pair, go] = dst
 
-        def quant_y(c, go):
-            first, count = CHUNKS[c]
-            span = slice(first * P, (first + count) * P)
-            codes = work.tile([P, count * P], U32, name="y_codes%d_%d" % (c, go), tag="y_codes", bufs=3, align_bytes=64)
-            nc.vector.quantize_mx(out=codes[:].bitcast(FP8X4), scales=y_scale[:, go, span], in_=y_bf[c, go][:])
+        def store_scales(scale, span):
+            for q in range(QUADRANTS):
+                nc.sync.dma_start(
+                    out=out_2[:, 4 * q : 4 * q + 4, span].rearrange("g r m -> r g m").bitcast(I32),
+                    in_=scale[32 * q : 32 * q + 4, :, :].bitcast(I32),
+                )
+
+        def quant_y(pair, go):
+            span = slice(pair * PAIR_TOKENS, (pair + 1) * PAIR_TOKENS)
+            scale = y_scale_last[:, go, :] if pair == PAIRS - 1 else y_scale_early[:, go, span]
+            codes = work.tile(
+                [P, PAIR_TOKENS], U32, name="y_codes%d_%d" % (pair, go), tag="y_codes", bufs=3, align_bytes=64
+            )
+            nc.vector.quantize_mx(out=codes[:].bitcast(FP8X4), scales=scale, in_=y_bf[pair, go][:])
             nc.sync.dma_start(
                 out=out_1[go, :, span, :].rearrange("p m t -> p (m t)").bitcast(I32), in_=codes[:].bitcast(I32)
             )
+            if (pair, go) == (PAIRS - 2, GROUPS - 1):
+                store_scales(y_scale_early, slice(0, early))
 
-        def turn_y(i, go):
-            c = chunk_of[i]
-            n = i - CHUNKS[c][0]
-            bank = next_bank()
-            for t in range(PACK):
-                nc.tensor.transpose(bank[:, t * P : (t + 1) * P], y_t[c, go][:, t, n * P : (n + 1) * P], ident[:])
-            y_bank[i, go] = bank
+        def turn_y(pair, go):
+            for n in range(PAIR):
+                bank = next_bank()
+                for t in range(SLOTS):
+                    nc.tensor.transpose(bank[:, t * P : (t + 1) * P], y_t[pair, go][:, t, n * P : (n + 1) * P], ident[:])
+                y_bank[pair, go, n] = bank
 
-        def copy_y(i, go, on_vector):
-            rows = work.tile([P, GROUP], F32, name="y_rows%d_%d" % (i, go), tag="y_rows", bufs=7)
-            dst = rows[:].rearrange("p (m t) -> p m t", t=PACK)
-            src = y_bank[i, go][:].rearrange("p (t m) -> p m t", t=PACK)
-            if on_vector:
-                nc.vector.tensor_copy(out=dst, in_=src)
-            else:
-                nc.scalar.copy(out=dst, in_=src)
-            nc.sync.dma_start(out=out_0[i * P : (i + 1) * P, go * GROUP : (go + 1) * GROUP], in_=rows[:])
+        def copy_y(pair, go):
+            for n in range(PAIR):
+                i = pair * PAIR + n
+                rows = work.tile([P, GROUP], F32, name="y_rows%d_%d" % (i, go), tag="y_rows", bufs=7)
+                nc.scalar.copy(
+                    out=rows[:].rearrange("p (m t) -> p m t", t=SLOTS),
+                    in_=y_bank[pair, go, n][:].rearrange("p (t m) -> p m t", t=SLOTS),
+                )
+                nc.sync.dma_start(out=out_0[i * P : (i + 1) * P, go * GROUP : (go + 1) * GROUP], in_=rows[:])
 
-        c2_jobs = [("c2", g, go) for g in range(GROUPS) for go in range(GROUPS)]
-        probe_jobs = [("probes", g, go) for go in range(GROUPS) for g in range(GROUPS)]
-        halves = [job + (half,) for job in c2_jobs + probe_jobs for half in range(2)]
-        constants = [constants_c, constants_d, constants_e]
-        to_multiply = [(c, h) for c in range(len(CHUNKS)) for h in range(2 * CHUNKS[c][1])]
-        to_weigh = []
-        to_turn = []
-        to_round = []
-        sorted_in = {}
-        rounded = {}
-        to_quant_y = []
-        rest = []
+        quarters = [("c2", g, go) for g in range(GROUPS) for go in range(GROUPS)]
+        quarters.extend(("probes", g, go) for go in range(GROUPS) for g in range(GROUPS))
+        probe_steps = [invert_guess_and_sign, newton_quotient, newton_sum]
 
-        def rounded_y(i, go, where):
-            round_y(i, go, where)
-            c = chunk_of[i]
-            rounded[c, go] = rounded.get((c, go), 0) + 1
-            if rounded[c, go] == CHUNKS[c][1]:
-                to_quant_y.append((c, go))
+        def third(r):
+            return [(pair, go) for pair in range(PAIRS) for go in range(GROUPS) if third_round(pair, go) == r]
 
-        constants_a()
-        order_c1_codes(0, 0)
-        constants_b()
-        order_c1_codes(1, 0)
-        order_c1_scale(0)
+        def is_tile(i):
+            return 0 <= i < TILES
+
+        take_abs()
+        sort_c1_codes(0, 0)
+        guess_root()
+        sort_c1_codes(1, 0)
         for i in range(2):
             turn_x(i)
             copy_x(i)
-        order_c1_codes(0, 1)
+        sort_c1_codes(0, 1)
+        sort_c1_codes(1, 1)
+        sort_c1_scale(0)
         quant_x(0)
-        order_c1_codes(1, 1)
-        order_c1_scale(1)
+        sort_c1_scale(1)
 
-        r = 0
-        while to_multiply or to_weigh or to_turn or to_round or to_quant_y:
-            j = r - LAG2
-            if r + 1 < TILES:
+        for r in range(third_round(PAIRS - 1, GROUPS - 1) + 4):
+            second = r - LAG2
+
+            if is_tile(r + 1):
                 quant_x(r + 1)
-            if 0 <= j - 1 < TILES:
-                quant2(j - 1, 0)
-            for job in rest:
-                round1(*job)
-            rest = []
-            for c, go in to_quant_y:
-                quant_y(c, go)
-            to_quant_y.clear()
-            if r < len(constants):
-                constants[r]()
-            if 0 <= j - 1 < TILES and QA == 0:
-                quant2(j - 1, 1)
-            turn_now = (B if r > A else 2)
-            turning = to_turn[:turn_now]
-            to_turn = to_turn[turn_now:]
-            on_v = (J if r >= C else E)
-            on_s = (0 if r >= C else 2 - E)
-            for i, go in to_round[:on_v]:
-                rounded_y(i, go, True)
-            to_round = to_round[on_v:]
-            if 0 <= j - 1 < TILES and QA == 1:
-                quant2(j - 1, 1)
-            s_round = to_round[:on_s]
-            to_round = to_round[on_s:]
-            for job in sorted_in.get(r - G, []):
-                quant_w(*job)
-            if 0 <= r - 1 < TILES:
+            if is_tile(second - 1):
+                quant2(second - 1, 0)
+            if is_tile(r - 1) and gpsimd_columns(r - 1) < K:
+                round1_on_vector(r - 1)
+            for pair, go in third(r - 3):
+                quant_y(pair, go)
+            if r < len(probe_steps):
+                probe_steps[r]()
+            if is_tile(second - 1):
+                quant2(second - 1, 1)
+            if r >= TILES:
+                for pair, go in third(r - 2):
+                    round_y(pair, go, nc.vector.tensor_copy)
+            if 0 <= r - 1 < len(quarters):
+                quant_w(*quarters[r - 1])
+            if is_tile(r - 1):
                 quant1(r - 1)
-            for c, h in to_weigh:
-                weigh(c, h)
-                go, t = slots(c, h)[-1]
-                if t == PACK - 1:
-                    first, count = CHUNKS[c]
-                    to_turn.extend((first + n, go) for n in range(count))
-                    on_g = I if j < TILES else 0
-                    for n in range(on_g):
-                        rounded_y(first + n, go, 2)
-                    to_round.extend((first + n, go) for n in range(on_g, count))
-            to_weigh = []
-            if r + 2 < TILES:
+            for pair, go in third(r - 1):
+                weigh(pair, go)
+
+            if is_tile(r + 2):
                 turn_x(r + 2)
-            for i, go in turning:
-                turn_y(i, go)
-            if r + 2 < TILES:
+            for pair, go in third(r - 2):
+                turn_y(pair, go)
+            if is_tile(r + 2):
                 copy_x(r + 2)
-            for n, (i, go) in enumerate(turning):
-                copy_y(i, go, (r >= D and n == 0))
-            if r < TILES:
+            for pair, go in third(r - 2):
+                copy_y(pair, go)
+
+            if is_tile(r):
                 for go in range(GROUPS):
-                    mm1(r, go)
-            if 0 <= j < TILES:
+                    multiply1(r, go)
+            if is_tile(second):
                 for go in range(GROUPS):
-                    mm2(j, go)
-            for n in range((B if r >= A else 2)):
-                if to_multiply:
-                    c, h = to_multiply[0]
-                    if sum(CHUNKS[c]) <= j and ("probes", 1, slots(c, h)[-1][0]) in w_codes:
-                        to_multiply = to_multiply[1:]
-                        mm3(c, h)
-                        to_weigh.append((c, h))
-            if r < TILES:
+                    multiply2(second, go)
+            for pair, go in third(r):
+                multiply3(pair, go)
+
+            if is_tile(r):
                 for go in range(GROUPS):
                     add1(r, go)
-            if 0 <= j < TILES:
+            if is_tile(second):
                 for go in range(GROUPS):
-                    add2(j, go)
-            if r < TILES:
-                cuts = GP_LATE if j >= 0 else GP_EARLY
-                for n in range(len(cuts) - 1):
-                    round1(r, cuts[n], cuts[n + 1], True)
-                if cuts[-1] < K:
-                    if REST_ON_VECTOR:
-                        rest.append((r, cuts[-1], K, False))
-                    else:
-                        round1(r, cuts[-1], K, False)
-            for i, go in s_round:
-                rounded_y(i, go, False)
-            sort_now = (F if len(halves) > 4 else H)
-            for job in halves[:sort_now]:
-                sort_w(*job, False)
-                if job[3] == 1:
-                    sorted_in.setdefault(r, []).append(job[:3])
-            halves = halves[sort_now:]
-            for c, h in to_weigh:
-                square(c, h)
-            r = r + 1
+                    add2(second, go)
+            if is_tile(r):
+                round1_on_gpsimd(r)
 
-        for q in range(4):
-            nc.sync.dma_start(
-                out=out_2[:, 4 * q : 4 * q + 4, :].rearrange("g r m -> r g m").bitcast(I32),
-                in_=y_scale[32 * q : 32 * q + 4, :, :].bitcast(I32),
-            )
+            if r < TILES:
+                for pair, go in third(r - 2):
+                    round_y(pair, go, nc.scalar.copy)
+            if r < len(quarters):
+                sort_w(*quarters[r])
+            for pair, go in third(r):
+                square(pair, go)
+
+        store_scales(y_scale_last, slice(early, M))

@@ -29,6 +29,7 @@ PAIR_TOKENS = PAIR * P
 PAIRS = TILES // PAIR
 X_LOADS = [(0, 1), (1, 2), (3, 2), (5, 3), (8, 4)]
 LAG2 = 5
+GPSIMD_COLUMNS = 768
 TINY = 1.0e-30
 HUGE = 3.0e38
 
@@ -259,18 +260,17 @@ def tile_probe_leverage_keep_k1_kernel(
             span = slice(go * GROUP, (go + 1) * GROUP)
             add_residual(z1[i][:, span], bank1[i, go], x_t[i][:, span])
 
-        def gpsimd_columns(i):
-            return GROUP if i >= LAG2 else 0
-
         def round1_on_gpsimd(i):
-            for first in range(0, gpsimd_columns(i), GROUP):
-                span = slice(first, first + GROUP)
+            for span in (slice(0, GROUP), slice(GROUP, GPSIMD_COLUMNS)):
                 nc.gpsimd.tensor_scalar(
                     out=z1_bf[i][:, span], in0=z1[i][:, span], scalar1=1.0, scalar2=0.0, op0=ALU.mult, op1=ALU.add
                 )
 
-        def round1_on_vector(i):
-            nc.vector.tensor_copy(out=z1_bf[i][:, gpsimd_columns(i) :], in_=z1[i][:, gpsimd_columns(i) :])
+        def round1_rest(i):
+            if i < LAG2:
+                nc.vector.tensor_copy(out=z1_bf[i][:], in_=z1[i][:])
+            else:
+                nc.scalar.copy(out=z1_bf[i][:, GPSIMD_COLUMNS:], in_=z1[i][:, GPSIMD_COLUMNS:])
 
         def quant1(i):
             z1_q[i] = quant_tile(z1_bf[i], "z1", i, LAG2 + 2)
@@ -436,8 +436,8 @@ def tile_probe_leverage_keep_k1_kernel(
                 quant_x(r + 1)
             if is_tile(second - 1):
                 quant2(second - 1, 0)
-            if is_tile(r - 1) and gpsimd_columns(r - 1) < K:
-                round1_on_vector(r - 1)
+            if is_tile(r - 1):
+                round1_rest(r - 1)
             for pair, go in third(r - 3):
                 quant_y(pair, go)
             if r < len(probe_steps):
@@ -478,7 +478,7 @@ def tile_probe_leverage_keep_k1_kernel(
             if is_tile(second):
                 for go in range(GROUPS):
                     add2(second, go)
-            if is_tile(r):
+            if is_tile(r) and is_tile(second):
                 round1_on_gpsimd(r)
 
             if r < TILES:

from contextlib import ExitStack

import concourse.mybir as mybir
from concourse.masks import make_identity

M, K, N = 1536, 1024, 1024
FLOPS = 2 * M * K * (K + K + N)

F32 = mybir.dt.float32
BF16 = mybir.dt.bfloat16
U32 = mybir.dt.uint32
I32 = mybir.dt.int32
U8 = mybir.dt.uint8
FP8X4 = mybir.dt.float8_e4m3fn_x4
FP4X4 = mybir.dt.float4_e2m1fn_x4
ALU = mybir.AluOpType
ACT = mybir.ActivationFunctionType

P = 128
SLOTS = 4
GROUP = P * SLOTS
GROUPS = K // GROUP
TILES = M // P
BANKS = 8
BANK_F32 = 512
QUADRANTS = 4
PAIR = 2
PAIR_TOKENS = PAIR * P
PAIRS = TILES // PAIR
X_LOADS = [(0, 1), (1, 2), (3, 2), (5, 3), (8, 4)]
LAG2 = 5
GPSIMD_COLUMNS = 768
TINY = 1.0e-30
HUGE = 3.0e38


def third_round(pair, go):
    ready = LAG2 + PAIR * pair + PAIR
    return ready + go if ready < TILES else ready


def tile_probe_leverage_keep_k1_kernel(
    tc, x, c1_words, c1_scales, c2, probes, rate, vote, out_0, out_1, out_2
):
    nc = tc.nc
    with ExitStack() as ctx:
        keep = ctx.enter_context(tc.tile_pool(name="keep", bufs=1))
        work = ctx.enter_context(tc.tile_pool(name="work", bufs=2))
        psum = ctx.enter_context(tc.psum_pool(name="psum", bufs=1))
        ctx.enter_context(tc.manual_schedule())

        banks_taken = []

        def next_bank():
            n = len(banks_taken)
            banks_taken.append(n)
            return psum.tile([P, BANK_F32], F32, name="bank%d" % n, tag="bank%d" % (n % BANKS))

        ident = keep.tile([P, P], F32, name="ident")
        make_identity(nc, ident[:])

        c1_scale_raw = keep.tile([P, GROUPS, K], U8, name="c1_scale_raw", align_bytes=64)
        nc.vector.memset(c1_scale_raw[:].bitcast(I32), 0)

        x_rows = {}
        w_raw = {}

        def load_x(first, count):
            rows = keep.tile([P, count, K], BF16, name="x_rows%d" % first)
            nc.sync.dma_start(
                out=rows[:], in_=x[first * P : (first + count) * P, :].rearrange("(n p) k -> p n k", p=P)
            )
            for n in range(count):
                x_rows[first + n] = rows[:, n, :]

        def load_w(name, w, g):
            raw = keep.tile([P, SLOTS, K], BF16, name="%s_raw%d" % (name, g))
            nc.sync.dma_start(out=raw[:], in_=w[g * GROUP : (g + 1) * GROUP, :].rearrange("(p j) n -> p j n", j=SLOTS))
            w_raw[name, g] = raw

        c1_word_raw = keep.tile([P, GROUPS, 2 * K], U8, name="c1_word_raw")
        rate_sb = keep.tile([P, GROUPS, SLOTS], BF16, name="rate_sb")
        vote_sb = keep.tile([P, GROUPS, SLOTS], BF16, name="vote_sb")
        nc.sync.dma_start(out=rate_sb[:], in_=rate.rearrange("(g p t) -> p g t", g=GROUPS, t=SLOTS))
        nc.sync.dma_start(out=c1_word_raw[:].bitcast(I32), in_=c1_words.rearrange("g p b -> p g b").bitcast(I32))
        load_x(*X_LOADS[0])
        for q in range(QUADRANTS):
            nc.scalar.dma_start(
                out=c1_scale_raw[32 * q : 32 * q + 4, :, :].bitcast(I32),
                in_=c1_scales[:, 4 * q : 4 * q + 4, :].rearrange("g r n -> r g n").bitcast(I32),
            )
        load_x(*X_LOADS[1])
        load_w("c2", c2, 0)
        nc.sync.dma_start(out=vote_sb[:], in_=vote.rearrange("(g p t) -> p g t", g=GROUPS, t=SLOTS))
        load_x(*X_LOADS[2])
        load_w("c2", c2, 1)
        load_x(*X_LOADS[3])
        load_w("probes", probes, 0)
        load_w("probes", probes, 1)
        load_x(*X_LOADS[4])

        c1_codes = {}
        c1_scale = {}

        def sort_c1_codes(g, go):
            codes = keep.tile([P, 2 * GROUP], U8, name="c1_codes%d%d" % (g, go), align_bytes=64)
            nc.vector.tensor_copy(
                out=codes[:].rearrange("p (t a m b) -> p a t m b", t=SLOTS, m=8, b=2),
                in_=c1_word_raw[:, g, 2 * GROUP * go : 2 * GROUP * (go + 1)].rearrange(
                    "p (a m t b) -> p a t m b", t=SLOTS, m=8, b=2
                ),
            )
            c1_codes[g, go] = codes

        def sort_c1_scale(go):
            scale = keep.tile([P, GROUPS, GROUP], U8, name="c1_scale%d" % go, align_bytes=64)
            nc.vector.tensor_copy(
                out=scale[:].rearrange("p g (t a m) -> p g a t m", t=SLOTS, m=16),
                in_=c1_scale_raw[:, :, GROUP * go : GROUP * (go + 1)].rearrange(
                    "p g (a m t) -> p g a t m", t=SLOTS, m=16
                ),
            )
            c1_scale[go] = scale

        def probe_tile(name):
            return keep.tile([P, GROUPS * SLOTS], F32, name=name)

        root, cap, gain = probe_tile("root"), probe_tile("cap"), probe_tile("gain")
        rate_abs, rate_safe, rate_sign = probe_tile("rate_abs"), probe_tile("rate_safe"), probe_tile("rate_sign")
        guess, inverse, half_quotient = probe_tile("guess"), probe_tile("inverse"), probe_tile("half_quotient")
        rate_cols = rate_sb[:].rearrange("p g t -> p (g t)")
        vote_cols = vote_sb[:].rearrange("p g t -> p (g t)")

        def take_abs():
            nc.vector.scalar_tensor_tensor(
                out=rate_abs[:], in0=rate_cols, scalar=-1.0, in1=rate_cols, op0=ALU.mult, op1=ALU.max
            )

        def guess_root():
            nc.vector.tensor_scalar(out=rate_safe[:], in0=rate_abs[:], scalar1=TINY, scalar2=None, op0=ALU.max)
            nc.scalar.activation(out=guess[:], in_=rate_safe[:], func=ACT.Sqrt)
            nc.scalar.activation(out=rate_sign[:], in_=rate_cols, func=ACT.Sign)

        def invert_guess_and_sign():
            nc.vector.reciprocal(out=inverse[:], in_=guess[:])
            nc.vector.tensor_scalar(out=cap[:], in0=rate_sign[:], scalar1=-HUGE, scalar2=1.0, op0=ALU.mult, op1=ALU.max)
            nc.vector.tensor_tensor(out=gain[:], in0=vote_cols, in1=rate_sign[:], op=ALU.mult)

        def newton_quotient():
            nc.vector.scalar_tensor_tensor(
                out=half_quotient[:], in0=rate_abs[:], scalar=0.5, in1=inverse[:], op0=ALU.mult, op1=ALU.mult
            )

        def newton_sum():
            nc.vector.scalar_tensor_tensor(
                out=root[:], in0=guess[:], scalar=0.5, in1=half_quotient[:], op0=ALU.mult, op1=ALU.add
            )

        w_sorted = {}
        w_codes = {}
        w_scale = {}

        def sort_w(name, g, go):
            dst = work.tile(
                [P, GROUP * SLOTS], BF16, name="w_sorted_%s%d%d" % (name, g, go), tag="w_sorted", bufs=3, align_bytes=64
            )
            nc.scalar.copy(
                out=dst[:].rearrange("p (t a i j) -> p a t i j", t=SLOTS, i=2, j=SLOTS),
                in_=w_raw[name, g][:, :, GROUP * go : GROUP * (go + 1)].rearrange(
                    "p j (a i t) -> p a t i j", t=SLOTS, i=2
                ),
            )
            w_sorted[name, g, go] = dst

        def quant_w(name, g, go):
            codes = keep.tile([P, GROUP], U32, name="%s_codes%d%d" % (name, g, go), align_bytes=64)
            scale = keep.tile([P, GROUP], U8, name="%s_scale%d%d" % (name, g, go), align_bytes=64)
            nc.vector.quantize_mx(out=codes[:].bitcast(FP8X4), scales=scale[:], in_=w_sorted[name, g, go][:])
            w_codes[name, g, go] = codes
            w_scale[name, g, go] = scale

        x_bank = {}
        x_t = {}
        x_q = {}

        def turn_x(i):
            bank = next_bank()
            words = x_rows[i].bitcast(F32)
            half = GROUP // 2
            for g in range(GROUPS):
                for u in range(2):
                    n = 2 * g + u
                    nc.tensor.transpose(bank[:, n * P : (n + 1) * P], words[:, half * g + u : half * (g + 1) : 2], ident[:])
            x_bank[i] = bank

        def copy_x(i):
            dst = work.tile([P, K], BF16, name="x_t%d" % i, tag="x_t", bufs=4, align_bytes=64)
            nc.scalar.copy(
                out=dst[:].bitcast(F32).rearrange("p (g r u) -> p g r u", g=GROUPS, u=2),
                in_=x_bank[i][:].rearrange("p (g u r) -> p g r u", g=GROUPS, u=2),
            )
            x_t[i] = dst

        def quant_tile(src, label, i, depth):
            codes = work.tile(
                [P, GROUPS * P], U32, name="%s_codes%d" % (label, i), tag=label + "_codes", bufs=depth, align_bytes=64
            )
            scale = work.tile(
                [P, GROUPS * P], U8, name="%s_scale%d" % (label, i), tag=label + "_scale", bufs=depth, align_bytes=64
            )
            nc.vector.quantize_mx(out=codes[:].bitcast(FP8X4), scales=scale[:], in_=src[:])
            return codes, scale

        def quant_x(i):
            x_q[i] = quant_tile(x_t[i], "x", i, 4)

        bank1 = {}
        bank2 = {}
        z1 = {}
        z1_bf = {}
        z1_q = {}
        z2_bf = {}
        z2_q = {}

        def multiply_tile(operand, weight, weight_scale):
            bank = next_bank()
            codes, scale = operand
            for t in range(SLOTS):
                for g in range(GROUPS):
                    nc.tensor.matmul_mx(
                        out=bank[:, t * P : (t + 1) * P],
                        lhsT=weight(g, t),
                        lhsT_scale=weight_scale(g, t),
                        rhs=codes[:, g * P : (g + 1) * P].bitcast(FP8X4),
                        rhs_scale=scale[:, g * P : (g + 1) * P],
                        start=(g == 0),
                        stop=(g == GROUPS - 1),
                    )
            return bank

        def add_residual(dst, bank, residual):
            nc.vector.tensor_tensor(
                out=dst.rearrange("p (r t) -> p r t", t=SLOTS),
                in0=bank[:].rearrange("p (t r) -> p r t", t=SLOTS),
                in1=residual.rearrange("p (r t) -> p r t", t=SLOTS),
                op=ALU.add,
            )

        def multiply1(i, go):
            bank1[i, go] = multiply_tile(
                x_q[i],
                lambda g, t: c1_codes[g, go][:, 2 * t * P : 2 * (t + 1) * P].bitcast(FP4X4),
                lambda g, t: c1_scale[go][:, g, t * P : (t + 1) * P],
            )

        def add1(i, go):
            if go == 0:
                z1[i] = work.tile([P, K], F32, name="z1_%d" % i, tag="z1", bufs=LAG2 + 2)
                z1_bf[i] = work.tile([P, K], BF16, name="z1_bf%d" % i, tag="z1_bf", bufs=3, align_bytes=64)
            span = slice(go * GROUP, (go + 1) * GROUP)
            add_residual(z1[i][:, span], bank1[i, go], x_t[i][:, span])

        def round1_on_gpsimd(i):
            for span in (slice(0, GROUP), slice(GROUP, GPSIMD_COLUMNS)):
                nc.gpsimd.tensor_scalar(
                    out=z1_bf[i][:, span], in0=z1[i][:, span], scalar1=1.0, scalar2=0.0, op0=ALU.mult, op1=ALU.add
                )

        def round1_rest(i):
            if i < LAG2:
                nc.vector.tensor_copy(out=z1_bf[i][:], in_=z1[i][:])
            else:
                nc.scalar.copy(out=z1_bf[i][:, GPSIMD_COLUMNS:], in_=z1[i][:, GPSIMD_COLUMNS:])

        def quant1(i):
            z1_q[i] = quant_tile(z1_bf[i], "z1", i, LAG2 + 2)

        def multiply2(i, go):
            bank2[i, go] = multiply_tile(
                z1_q[i],
                lambda g, t: w_codes["c2", g, go][:, t * P : (t + 1) * P].bitcast(FP8X4),
                lambda g, t: w_scale["c2", g, go][:, t * P : (t + 1) * P],
            )

        def add2(i, go):
            dst = work.tile([P, GROUP], BF16, name="z2_bf%d_%d" % (i, go), tag="z2_bf", bufs=4, align_bytes=64)
            add_residual(dst[:], bank2[i, go], z1[i][:, go * GROUP : (go + 1) * GROUP])
            z2_bf[i, go] = dst

        def quant2(i, g):
            pair, n = divmod(i, PAIR)
            if n == 0:
                codes = work.tile(
                    [P, PAIR_TOKENS], U32, name="z2_codes%d_%d" % (pair, g), tag="z2_codes", bufs=6, align_bytes=64
                )
                scale = work.tile(
                    [P, PAIR_TOKENS], U8, name="z2_scale%d_%d" % (pair, g), tag="z2_scale", bufs=6, align_bytes=64
                )
                z2_q[pair, g] = (codes, scale)
            codes, scale = z2_q[pair, g]
            span = slice(n * P, (n + 1) * P)
            nc.vector.quantize_mx(out=codes[:, span].bitcast(FP8X4), scales=scale[:, span], in_=z2_bf[i, g][:])

        slots_in_bank = BANK_F32 // PAIR_TOKENS
        bank3 = {}
        energy = {}
        y_t = {}
        y_bf = {}
        y_bank = {}
        early = M - PAIR_TOKENS
        y_scale_early = keep.tile([P, GROUPS, early], U8, name="y_scale_early", align_bytes=64)
        y_scale_last = keep.tile([P, GROUPS, PAIR_TOKENS], U8, name="y_scale_last", align_bytes=64)

        def slot_span(t):
            n = t % slots_in_bank
            return slice(n * PAIR_TOKENS, (n + 1) * PAIR_TOKENS)

        def multiply3(pair, go):
            for t in range(SLOTS):
                if t % slots_in_bank == 0:
                    bank = next_bank()
                for g in range(GROUPS):
                    codes, scale = z2_q[pair, g]
                    nc.tensor.matmul_mx(
                        out=bank[:, slot_span(t)],
                        lhsT=w_codes["probes", g, go][:, t * P : (t + 1) * P].bitcast(FP8X4),
                        lhsT_scale=w_scale["probes", g, go][:, t * P : (t + 1) * P],
                        rhs=codes[:].bitcast(FP8X4),
                        rhs_scale=scale[:],
                        start=(g == 0),
                        stop=(g == GROUPS - 1),
                    )
                bank3[pair, go, t] = bank

        def square(pair, go):
            for t in range(SLOTS):
                if t % slots_in_bank == 0:
                    dst = work.tile([P, BANK_F32], F32, name="energy%d_%d_%d" % (pair, go, t), tag="energy", bufs=4)
                col = go * SLOTS + t
                nc.scalar.activation(
                    out=dst[:, slot_span(t)],
                    in_=bank3[pair, go, t][:, slot_span(t)],
                    func=ACT.Square,
                    scale=root[:, col : col + 1],
                )
                energy[pair, go, t] = dst

        def weigh(pair, go):
            dst = work.tile([P, SLOTS, PAIR_TOKENS], F32, name="y_t%d_%d" % (pair, go), tag="y_t", bufs=4)
            for t in range(SLOTS):
                col = go * SLOTS + t
                nc.vector.tensor_scalar(
                    out=dst[:, t, :],
                    in0=energy[pair, go, t][:, slot_span(t)],
                    scalar1=cap[:, col : col + 1],
                    scalar2=gain[:, col : col + 1],
                    op0=ALU.min,
                    op1=ALU.mult,
                )
            y_t[pair, go] = dst

        def round_y(pair, go, copy):
            dst = work.tile(
                [P, PAIR_TOKENS * SLOTS], BF16, name="y_bf%d_%d" % (pair, go), tag="y_bf", bufs=3, align_bytes=64
            )
            copy(
                out=dst[:].rearrange("p (a i t) -> p a t i", t=SLOTS, i=4),
                in_=y_t[pair, go][:].rearrange("p t (a i) -> p a t i", i=4),
            )
            y_bf[pair, go] = dst

        def store_scales(scale, span):
            for q in range(QUADRANTS):
                nc.sync.dma_start(
                    out=out_2[:, 4 * q : 4 * q + 4, span].rearrange("g r m -> r g m").bitcast(I32),
                    in_=scale[32 * q : 32 * q + 4, :, :].bitcast(I32),
                )

        def quant_y(pair, go):
            span = slice(pair * PAIR_TOKENS, (pair + 1) * PAIR_TOKENS)
            scale = y_scale_last[:, go, :] if pair == PAIRS - 1 else y_scale_early[:, go, span]
            codes = work.tile(
                [P, PAIR_TOKENS], U32, name="y_codes%d_%d" % (pair, go), tag="y_codes", bufs=3, align_bytes=64
            )
            nc.vector.quantize_mx(out=codes[:].bitcast(FP8X4), scales=scale, in_=y_bf[pair, go][:])
            nc.sync.dma_start(
                out=out_1[go, :, span, :].rearrange("p m t -> p (m t)").bitcast(I32), in_=codes[:].bitcast(I32)
            )
            if (pair, go) == (PAIRS - 2, GROUPS - 1):
                store_scales(y_scale_early, slice(0, early))

        def turn_y(pair, go):
            for n in range(PAIR):
                bank = next_bank()
                for t in range(SLOTS):
                    nc.tensor.transpose(bank[:, t * P : (t + 1) * P], y_t[pair, go][:, t, n * P : (n + 1) * P], ident[:])
                y_bank[pair, go, n] = bank

        def copy_y(pair, go):
            for n in range(PAIR):
                i = pair * PAIR + n
                rows = work.tile([P, GROUP], F32, name="y_rows%d_%d" % (i, go), tag="y_rows", bufs=7)
                nc.scalar.copy(
                    out=rows[:].rearrange("p (m t) -> p m t", t=SLOTS),
                    in_=y_bank[pair, go, n][:].rearrange("p (t m) -> p m t", t=SLOTS),
                )
                nc.sync.dma_start(out=out_0[i * P : (i + 1) * P, go * GROUP : (go + 1) * GROUP], in_=rows[:])

        quarters = [("c2", g, go) for g in range(GROUPS) for go in range(GROUPS)]
        quarters.extend(("probes", g, go) for go in range(GROUPS) for g in range(GROUPS))
        probe_steps = [invert_guess_and_sign, newton_quotient, newton_sum]

        def third(r):
            return [(pair, go) for pair in range(PAIRS) for go in range(GROUPS) if third_round(pair, go) == r]

        def is_tile(i):
            return 0 <= i < TILES

        take_abs()
        sort_c1_codes(0, 0)
        guess_root()
        sort_c1_codes(1, 0)
        for i in range(2):
            turn_x(i)
            copy_x(i)
        sort_c1_codes(0, 1)
        sort_c1_codes(1, 1)
        sort_c1_scale(0)
        quant_x(0)
        sort_c1_scale(1)

        for r in range(third_round(PAIRS - 1, GROUPS - 1) + 4):
            second = r - LAG2

            if is_tile(r + 1):
                quant_x(r + 1)
            if is_tile(second - 1):
                quant2(second - 1, 0)
            if is_tile(r - 1):
                round1_rest(r - 1)
            for pair, go in third(r - 3):
                quant_y(pair, go)
            if r < len(probe_steps):
                probe_steps[r]()
            if is_tile(second - 1):
                quant2(second - 1, 1)
            if r >= TILES:
                for pair, go in third(r - 2):
                    round_y(pair, go, nc.vector.tensor_copy)
            if 0 <= r - 1 < len(quarters):
                quant_w(*quarters[r - 1])
            if is_tile(r - 1):
                quant1(r - 1)
            for pair, go in third(r - 1):
                weigh(pair, go)

            if is_tile(r + 2):
                turn_x(r + 2)
            for pair, go in third(r - 2):
                turn_y(pair, go)
            if is_tile(r + 2):
                copy_x(r + 2)
            for pair, go in third(r - 2):
                copy_y(pair, go)

            if is_tile(r):
                for go in range(GROUPS):
                    multiply1(r, go)
            if is_tile(second):
                for go in range(GROUPS):
                    multiply2(second, go)
            for pair, go in third(r):
                multiply3(pair, go)

            if is_tile(r):
                for go in range(GROUPS):
                    add1(r, go)
            if is_tile(second):
                for go in range(GROUPS):
                    add2(second, go)
            if is_tile(r) and is_tile(second):
                round1_on_gpsimd(r)

            if r < TILES:
                for pair, go in third(r - 2):
                    round_y(pair, go, nc.scalar.copy)
            if r < len(quarters):
                sort_w(*quarters[r])
            for pair, go in third(r):
                square(pair, go)

        store_scales(y_scale_last, slice(early, M))
